import numpy as np
import ml_dtypes


def mxq(x, axis, fmt="e4m3"):
    dtype, down = {"e4m3": (ml_dtypes.float8_e4m3fn, 7), "e5m2": (ml_dtypes.float8_e5m2, 14)}[fmt]
    v = np.moveaxis(np.asarray(x, np.float32).astype(ml_dtypes.bfloat16).astype(np.float64), axis, -1)
    blocks = v.reshape(v.shape[:-1] + (-1, 32))
    amax = np.abs(blocks).max(-1, keepdims=True)
    byte = np.maximum(np.where(amax > 0, np.frexp(amax)[1] - 1 + 127, 0) - down, 1)
    scale = np.exp2(byte - 127.0)
    codes = (blocks / scale).astype(np.float32).astype(dtype).astype(np.float64)
    return np.moveaxis((codes * scale).reshape(v.shape), -1, axis)


WIDE = False


def mx_kscale(k):
    if not WIDE:
        return np.ones(k)
    levels = np.array([10, -10, 5, -5, 0])
    if k % 512:
        return np.exp2(np.random.permutation(np.resize(levels, k // 32))).repeat(32)
    a = np.empty((k // 512, 16))
    for p in range(k // 512):
        a[p, :8] = np.random.permutation(np.resize(levels, 8))
        for g in range(8):
            far = levels[np.abs(levels - a[p, g]) >= 10]
            a[p, g + 8] = far[np.random.randint(len(far))]
    return np.exp2(a.ravel()).repeat(32)


def f64(x):
    return np.asarray(x).astype(np.float64)


def striped(idx):
    return np.tile(idx.reshape(-1, 16).T, (8, 1)).astype(np.uint16)


def unstriped(offs):
    return offs[:16].T.reshape(-1).astype(np.int64)


def pack_weight(w):
    k, n = w.shape
    w = f64(np.asarray(w, np.float32).astype(ml_dtypes.bfloat16)).reshape(k // 32, 32, n)
    amax = np.abs(w).max(1)
    byte = np.clip(np.where(amax > 0, np.frexp(amax)[1] - 1 + 127 - 7, 1), 1, 254)
    scaled = (w * np.exp2(127.0 - byte)[:, None, :]).reshape(k, n).astype(np.float32)
    words = np.ascontiguousarray(scaled.reshape(k // 512, 128, 4, n).transpose(0, 1, 3, 2)).astype(ml_dtypes.float8_e4m3fn).view(np.uint8)
    return words, np.ascontiguousarray(byte.astype(np.uint8).reshape(k // 512, 16, n))


def unpack_weight(words, scales):
    g, p, n, _ = words.shape
    vals = np.ascontiguousarray(words).view(ml_dtypes.float8_e4m3fn).astype(np.float64) * np.repeat(np.exp2(scales.astype(np.float64) - 127.0), 8, axis=1)[..., None]
    return vals.transpose(0, 1, 3, 2).reshape(g * 512, n)


E2M1 = np.array([0.0, 0.5, 1.0, 1.5, 2.0, 3.0, 4.0, 6.0, -0.0, -0.5, -1.0, -1.5, -2.0, -3.0, -4.0, -6.0])


def pack_fp4(w):
    k, n = w.shape
    w = f64(np.asarray(w, np.float32).astype(ml_dtypes.bfloat16)).reshape(k // 32, 32, n)
    amax = np.abs(w).max(1)
    mant, ex = np.frexp(amax / 6.0)
    byte = np.clip(np.where(amax > 0, np.where(mant > 0.5, ex, ex - 1) + 127, 1), 1, 254)
    scaled = (w * np.exp2(127.0 - byte)[:, None, :]).reshape(k, n).astype(np.float32)
    c = np.ascontiguousarray(scaled.reshape(k // 512, 128, 4, n).transpose(0, 1, 3, 2)).astype(ml_dtypes.float4_e2m1fn).view(np.uint8) & 0xF
    words = (c[..., 0::2] | (c[..., 1::2] << 4)).reshape(k // 512, 128, 2 * n)
    return np.ascontiguousarray(words), np.ascontiguousarray(byte.astype(np.uint8).reshape(k // 512, 16, n))


def unpack_fp4(words, scales):
    g, _, n = scales.shape
    words = np.ascontiguousarray(words).reshape(g, 128, n, 2)
    nib = np.empty((g, 128, n, 4), np.uint8)
    nib[..., 0::2] = words & 0xF
    nib[..., 1::2] = words >> 4
    vals = E2M1[nib] * np.repeat(np.exp2(scales.astype(np.float64) - 127.0), 8, axis=1)[..., None]
    return vals.transpose(0, 1, 3, 2).reshape(g * 512, n)


def gelu(v):
    return 0.5 * v * (1.0 + np.tanh(np.sqrt(2.0 / np.pi) * (v + 0.044715 * v**3)))


K, T, S, H, N = 1024, 1024, 512, 512, 256
P = 2 ** 7


def setup_inputs():
    n = np.random.standard_normal
    s = mx_kscale(K)[:, None]
    u = mx_kscale(H)
    packed_xT = pack_weight(n((K, T)) * s)
    packed_w2 = pack_fp4(n((H, N)) / np.sqrt(H) / u[:, None])
    return {
        "x_words": packed_xT[0],
        "x_scales": packed_xT[1],
        "gate": np.tile(np.random.uniform(0.2, 1.0, S), (P, 1)).astype(np.float32),
        "res": n((N, T)).astype(np.float32),
        "w1": (n((K, H)) / np.sqrt(K) / s * u).astype(np.float32),
        "w2_words": packed_w2[0],
        "w2_scales": packed_w2[1],
        "offs": striped(np.random.permutation(T)[:S]),
    }


def reference(x_words, x_scales, gate, res, w1, w2_words, w2_scales, offs):
    r = f64(res)[:, unstriped(offs)]
    xq = unpack_weight(x_words, x_scales)[:, unstriped(offs)]
    h = gelu(mxq(f64(w1), 0, "e4m3").T @ xq)
    y = unpack_fp4(w2_words, w2_scales).T @ mxq(h, 0, "e4m3")
    out = f64(res).copy()
    out[:, unstriped(offs)] = r + y * f64(gate)[:1]
    return out

@@ -1,0 +1,229 @@
+from contextlib import ExitStack
+
+import concourse.mybir as mybir
+from concourse.masks import make_identity
+
+K, T, S, H, N = 1024, 1024, 512, 512, 256
+P = 128
+PACK = 4
+PASSES = K // (P * PACK)
+CHUNK = 128
+HALF = S // 2
+FLOPS = 2 * S * (K * H + H * N)
+
+F32 = mybir.dt.float32
+BF16 = mybir.dt.bfloat16
+I32 = mybir.dt.int32
+U32 = mybir.dt.uint32
+U16 = mybir.dt.uint16
+U8 = mybir.dt.uint8
+FP8X4 = mybir.dt.float8_e4m3fn_x4
+FP4X4 = mybir.dt.float4_e2m1fn_x4
+GELU = mybir.ActivationFunctionType.Gelu_apprx_tanh
+COPY = mybir.ActivationFunctionType.Copy
+ADD = mybir.AluOpType.add
+MULT = mybir.AluOpType.mult
+
+
+def tile_picked_modres_mlpgelu_p_kernel(
+    tc, x_words, x_scales, gate, res, w1, w2_words, w2_scales, offs, out
+):
+    nc = tc.nc
+    with ExitStack() as ctx:
+        keep = ctx.enter_context(tc.tile_pool(name="keep", bufs=1))
+        stream = ctx.enter_context(tc.tile_pool(name="stream", bufs=1))
+        psum = ctx.enter_context(tc.psum_pool(name="psum", bufs=1))
+
+        def sb(name, shape, dtype, tag=None):
+            return keep.tile(shape, dtype, name=name, tag=tag or name, align_bytes=64)
+
+        def placed(name, shape, dtype, offset):
+            return stream.tile(shape, dtype, name=name, offset=offset, align_bytes=64)
+
+        offsets = sb("offsets", [P, S // 16], U16)
+        nc.sync.dma_start(offsets[:], offs)
+
+        def entries(lo, hi):
+            return offsets[:, lo // 16 : hi // 16]
+
+        xs_all = sb("xs_all", [P, T], U8)
+        nc.gpsimd.memset(xs_all[:].bitcast(I32), 0)
+        warm_in = placed("warm_in", [P, 32], F32, 8192 - 64)
+        warm_out = placed("warm_out", [P, 16], F32, 12288)
+        nc.vector.memset(warm_in[:], 0.0)
+        nc.scalar.activation(warm_out[:], warm_in[:, 0:16], GELU)
+
+        xw_all = []
+        for g in range(PASSES):
+            t = sb("xw_all%d" % g, [P, T], U32)
+            nc.sync.dma_start(t[:].bitcast(I32), x_words[g].rearrange("p n t -> p (n t)").bitcast(I32))
+            xw_all.append(t)
+        for q in range(4):
+            nc.sync.dma_start(
+                xs_all[32 * q : 32 * q + 8, :].bitcast(I32),
+                x_scales[:, 4 * q : 4 * q + 4, :].bitcast(I32),
+            )
+
+        w1_rows = w1.rearrange("(g p j) c -> g p j c", g=PASSES, j=PACK)
+        pieces = [(0, 0, H, 0), (1, 0, H // 2, 8192), (1, H // 2, H, 12288)]
+        raw = []
+        for i, (g, lo, hi, at) in enumerate(pieces):
+            t = placed("w1_raw%d" % i, [P, PACK, hi - lo], F32, at)
+            nc.sync.dma_start(t[:], w1_rows[g][:, :, lo:hi])
+            raw.append(t)
+
+        w2w = sb("w2w", [P, 2 * N], U8)
+        w2s = sb("w2s", [P, N], U8)
+        nc.gpsimd.memset(w2s[:].bitcast(I32), 0)
+        nc.gpsimd.dma_start(w2w[:].bitcast(I32), w2_words[0].bitcast(I32))
+        for q in range(4):
+            nc.gpsimd.dma_start(
+                w2s[32 * q : 32 * q + 4, :].bitcast(I32),
+                w2_scales[0][4 * q : 4 * q + 4, :].bitcast(I32),
+            )
+        ident = sb("ident", [P, P], F32)
+        make_identity(nc, ident[:])
+
+        xw = [sb("xw%d" % g, [P, S], U32) for g in range(PASSES)]
+        for g in range(PASSES):
+            nc.vector.tensor_copy(xw[g][:], xw_all[g][:].indirect(offsets[:]))
+        xs = sb("xs", [P, S], U8)
+        nc.vector.tensor_copy(xs[:], xs_all[:].indirect(offsets[:]))
+
+        rows = [sb("rows0", [P, T], F32, "xw_all0"), sb("rows1", [P, T], F32, "xs_all")]
+        nc.sync.dma_start(rows[0][:], res[0:P, :])
+        gate_sb = sb("gate_sb", [P, CHUNK], F32, "xw_all1")
+        nc.sync.dma_start(gate_sb[:], gate[:, 0:CHUNK])
+        gate_col = sb("gate_col", [P, S // P - 1], F32)
+        with nc.allow_non_contiguous_dma(reason="one gate value a partition"):
+            nc.gpsimd.dma_start(gate_col[:], gate[0, CHUNK:S].rearrange("(c p) -> p c", p=P))
+        nc.sync.dma_start(rows[1][:], res[P : 2 * P, :])
+
+        stage = [[sb("stage%d%d" % (g, u), [P, 2, P, PACK], BF16) for u in range(2)] for g in range(PASSES)]
+        w1q = [sb("w1q%d" % g, [P, H], U32) for g in range(PASSES)]
+        w1s = [sb("w1s%d" % g, [P, H], U8) for g in range(PASSES)]
+        for i, (g, lo, hi, at) in enumerate(pieces):
+            src = raw[i][:].rearrange("p j (m t) -> p m j t", t=PACK)
+            for u in range(2):
+                dst = stage[g][u][:, :, lo // PACK : hi // PACK, :].rearrange("p t m j -> p m j t")
+                if u == 0:
+                    nc.vector.tensor_copy(dst, src[:, :, :, 0:2])
+                else:
+                    nc.scalar.copy(dst, src[:, :, :, 2:4])
+            if hi == H:
+                for u in range(2):
+                    cols = slice(2 * P * u, 2 * P * (u + 1))
+                    nc.vector.quantize_mx(
+                        out=w1q[g][:, cols].bitcast(FP8X4),
+                        scales=w1s[g][:, cols],
+                        in_=stage[g][u][:].rearrange("p t m j -> p (t m j)"),
+                    )
+
+        old0 = sb("old0", [P, S], F32)
+        old1 = {}
+        hq = sb("hq", [P, S], U32)
+        hs = sb("hs", [P, S], U8)
+
+        def layer1(c):
+            cols = slice(CHUNK * c, CHUNK * (c + 1))
+            acc = psum.tile([P, PACK, CHUNK], F32, name="acc%d" % c)
+            for t in range(PACK):
+                m = slice(P * t, P * (t + 1))
+                for g in range(PASSES):
+                    nc.tensor.matmul_mx(
+                        out=acc[:, t, :],
+                        lhsT=w1q[g][:, m].bitcast(FP8X4),
+                        lhsT_scale=w1s[g][:, m],
+                        rhs=xw[g][:, cols].bitcast(FP8X4),
+                        rhs_scale=xs[4 * g : P, cols],
+                        start=(g == 0),
+                        stop=(g == PASSES - 1),
+                    )
+            h = sb("h%d" % c, [P, CHUNK, PACK], BF16)
+            nc.scalar.activation(h[:], acc[:].rearrange("p t n -> p n t"), GELU)
+            nc.vector.quantize_mx(
+                out=hq[:, cols].bitcast(FP8X4), scales=hs[:, cols], in_=h[:].rearrange("p n t -> p (n t)")
+            )
+
+        def layer2(lo, hi):
+            y = psum.tile([P, 2, hi - lo], F32, name="y%d" % lo, tag="y", bufs=2)
+            for b in range(2):
+                for c0 in range(lo, hi, CHUNK):
+                    nc.tensor.matmul_mx(
+                        out=y[:, b, c0 - lo : c0 - lo + CHUNK],
+                        lhsT=w2w[:, 2 * P * b : 2 * P * (b + 1)].bitcast(FP4X4),
+                        lhsT_scale=w2s[:, P * b : P * (b + 1)],
+                        rhs=hq[:, c0 : c0 + CHUNK].bitcast(FP8X4),
+                        rhs_scale=hs[:, c0 : c0 + CHUNK],
+                        start=True,
+                        stop=True,
+                    )
+            gy = sb("gy%d" % lo, [P, 2, hi - lo], F32)
+            nc.vector.tensor_tensor(
+                gy[:], y[:], gate_sb[:, lo:hi].unsqueeze(1).to_broadcast([P, 2, hi - lo]), MULT
+            )
+            return gy
+
+        gy_late = sb("gy_late", [P, 2, S - CHUNK], F32)
+
+        def layer2_turned(c):
+            cols = slice(CHUNK * c, CHUNK * (c + 1))
+            yt = psum.tile([P, N], F32, name="yt%d" % c, tag="y", bufs=2)
+            nc.tensor.matmul_mx(
+                out=yt[:],
+                lhsT=hq[:, cols].bitcast(FP8X4),
+                lhsT_scale=hs[:, cols],
+                rhs=w2w[:].bitcast(FP4X4),
+                rhs_scale=w2s[:],
+                start=True,
+                stop=True,
+            )
+            gyt = sb("gyt%d" % c, [P, N], F32)
+            nc.scalar.activation(gyt[:], yt[:], COPY, scale=gate_col[:, c - 1 : c])
+            back = psum.tile([P, 2, CHUNK], F32, name="back%d" % c, tag="back", bufs=2)
+            for b in range(2):
+                nc.tensor.transpose(back[:, b, :], gyt[:, P * b : P * (b + 1)], ident[:])
+            nc.scalar.copy(gy_late[:, :, CHUNK * (c - 1) : CHUNK * c], back[:])
+
+        def old_cols(b, lo, hi):
+            if b == 0:
+                return old0[:, lo:hi]
+            base = lo // HALF * HALF
+            return old1[base][:, lo - base : hi - base]
+
+        def fetch_old1(base, tag):
+            old1[base] = sb("old1_%d" % base, [P, HALF], F32, tag)
+            nc.vector.tensor_copy(old1[base][:], rows[1][:].indirect(entries(base, base + HALF)))
+
+        def put(vals, lo, hi, b):
+            nc.vector.tensor_tensor(rows[b][:].indirect(entries(lo, hi)), vals, old_cols(b, lo, hi), ADD)
+
+        for i in range(2):
+            warm_acc = psum.tile([P, S], F32, name="warm_acc%d" % i, tag="back", bufs=2)
+            nc.tensor.matmul_mx(
+                out=warm_acc[:],
+                lhsT=w1q[0][:, 0:P].bitcast(FP8X4),
+                lhsT_scale=w1s[0][:, 0:P],
+                rhs=xw[0][:].bitcast(FP8X4),
+                rhs_scale=xs[:],
+                start=True,
+                stop=True,
+            )
+        nc.vector.tensor_copy(old0[:], rows[0][:].indirect(offsets[:]))
+        layer1(0)
+        fetch_old1(HALF, "h0")
+        layer1(1)
+        gy0 = layer2(0, CHUNK)
+        layer1(2)
+        layer2_turned(1)
+        layer1(3)
+        fetch_old1(0, "h3")
+        layer2_turned(2)
+        layer2_turned(3)
+        for b in range(2):
+            put(gy0[:, b, :], 0, CHUNK, b)
+        put(gy_late[:, 0, 0:CHUNK], CHUNK, 2 * CHUNK, 0)
+        put(gy_late[:, 1, 0:CHUNK], CHUNK, 2 * CHUNK, 1)
+        for b in range(2):
+            put(gy_late[:, b, CHUNK:], 2 * CHUNK, S, b)
+            nc.sync.dma_start(out[P * b : P * (b + 1), :], rows[b][:])

@@ -1,7 +1,6 @@
 from contextlib import ExitStack
 
 import concourse.mybir as mybir
-from concourse.masks import make_identity
 
 K, T, S, H, N = 1024, 1024, 512, 512, 256
 P = 128
@@ -21,6 +20,7 @@ FP8X4 = mybir.dt.float8_e4m3fn_x4
 FP4X4 = mybir.dt.float4_e2m1fn_x4
 GELU = mybir.ActivationFunctionType.Gelu_apprx_tanh
 COPY = mybir.ActivationFunctionType.Copy
+IS_EQUAL = mybir.AluOpType.is_equal
 ADD = mybir.AluOpType.add
 MULT = mybir.AluOpType.mult
 
@@ -46,8 +46,16 @@ def tile_picked_modres_mlpgelu_p_kernel(
         def entries(lo, hi):
             return offsets[:, lo // 16 : hi // 16]
 
-        xs_all = sb("xs_all", [P, T], U8)
+        xs_all = placed("xs_all", [P, T], U8, 16768)
         nc.gpsimd.memset(xs_all[:].bitcast(I32), 0)
+        ones = sb("ones", [P, P], F32)
+        nc.vector.memset(ones[:], 1.0)
+        ident = sb("ident", [P, P], F32)
+        nc.gpsimd.affine_select(
+            out=ident[:], in_=ones[:], compare_op=IS_EQUAL, fill=0.0, base=0, pattern=[[-1, P]], channel_multiplier=1
+        )
+        w2s = sb("w2s", [P, N], U8, "ones")
+        nc.gpsimd.memset(w2s[:].bitcast(I32), 0)
         warm_in = placed("warm_in", [P, 32], F32, 8192 - 64)
         warm_out = placed("warm_out", [P, 16], F32, 12288)
         nc.vector.memset(warm_in[:], 0.0)
@@ -63,26 +71,19 @@ def tile_picked_modres_mlpgelu_p_kernel(
                 xs_all[32 * q : 32 * q + 8, :].bitcast(I32),
                 x_scales[:, 4 * q : 4 * q + 4, :].bitcast(I32),
             )
-
-        w1_rows = w1.rearrange("(g p j) c -> g p j c", g=PASSES, j=PACK)
-        pieces = [(0, 0, H, 0), (1, 0, H // 2, 8192), (1, H // 2, H, 12288)]
-        raw = []
-        for i, (g, lo, hi, at) in enumerate(pieces):
-            t = placed("w1_raw%d" % i, [P, PACK, hi - lo], F32, at)
-            nc.sync.dma_start(t[:], w1_rows[g][:, :, lo:hi])
-            raw.append(t)
-
-        w2w = sb("w2w", [P, 2 * N], U8)
-        w2s = sb("w2s", [P, N], U8)
-        nc.gpsimd.memset(w2s[:].bitcast(I32), 0)
-        nc.gpsimd.dma_start(w2w[:].bitcast(I32), w2_words[0].bitcast(I32))
         for q in range(4):
             nc.gpsimd.dma_start(
                 w2s[32 * q : 32 * q + 4, :].bitcast(I32),
                 w2_scales[0][4 * q : 4 * q + 4, :].bitcast(I32),
             )
-        ident = sb("ident", [P, P], F32)
-        make_identity(nc, ident[:])
+
+        w1_rows = w1.rearrange("(g p j) c -> g p j c", g=PASSES, j=PACK)
+        pieces = [(0, 0, H, 0, 2), (1, 0, H // 2, 8192, 1), (1, H // 2, H, 12288, 2)]
+        raw = []
+        for i, (g, lo, hi, at, share) in enumerate(pieces):
+            t = placed("w1_raw%d" % i, [P, PACK, hi - lo], F32, at)
+            nc.sync.dma_start(t[:], w1_rows[g][:, :, lo:hi])
+            raw.append(t)
 
         xw = [sb("xw%d" % g, [P, S], U32) for g in range(PASSES)]
         for g in range(PASSES):
@@ -90,33 +91,33 @@ def tile_picked_modres_mlpgelu_p_kernel(
         xs = sb("xs", [P, S], U8)
         nc.vector.tensor_copy(xs[:], xs_all[:].indirect(offsets[:]))
 
-        rows = [sb("rows0", [P, T], F32, "xw_all0"), sb("rows1", [P, T], F32, "xs_all")]
-        nc.sync.dma_start(rows[0][:], res[0:P, :])
-        gate_sb = sb("gate_sb", [P, CHUNK], F32, "xw_all1")
+        rows = [sb("rows%d" % b, [P, T], F32, "xw_all%d" % b) for b in range(2)]
+        for b in range(2):
+            nc.sync.dma_start(rows[b][:], res[P * b : P * (b + 1), :])
+        w2w = placed("w2w", [P, 2 * N], U8, 16768)
+        nc.sync.dma_start(w2w[:].bitcast(I32), w2_words[0].bitcast(I32))
+        gate_col = placed("gate_col", [P, S // P - 1], F32, 16768 + 512)
+        gate_sb = placed("gate_sb", [P, CHUNK], F32, 16768 + 576)
         nc.sync.dma_start(gate_sb[:], gate[:, 0:CHUNK])
-        gate_col = sb("gate_col", [P, S // P - 1], F32)
         with nc.allow_non_contiguous_dma(reason="one gate value a partition"):
-            nc.gpsimd.dma_start(gate_col[:], gate[0, CHUNK:S].rearrange("(c p) -> p c", p=P))
-        nc.sync.dma_start(rows[1][:], res[P : 2 * P, :])
+            nc.sync.dma_start(gate_col[:], gate[0, CHUNK:S].rearrange("(c p) -> p c", p=P))
 
-        stage = [[sb("stage%d%d" % (g, u), [P, 2, P, PACK], BF16) for u in range(2)] for g in range(PASSES)]
+        stage = [sb("stage%d" % g, [P, PACK, P, PACK], BF16) for g in range(PASSES)]
         w1q = [sb("w1q%d" % g, [P, H], U32) for g in range(PASSES)]
         w1s = [sb("w1s%d" % g, [P, H], U8) for g in range(PASSES)]
-        for i, (g, lo, hi, at) in enumerate(pieces):
+        for i, (g, lo, hi, at, share) in enumerate(pieces):
             src = raw[i][:].rearrange("p j (m t) -> p m j t", t=PACK)
-            for u in range(2):
-                dst = stage[g][u][:, :, lo // PACK : hi // PACK, :].rearrange("p t m j -> p m j t")
-                if u == 0:
-                    nc.vector.tensor_copy(dst, src[:, :, :, 0:2])
-                else:
-                    nc.scalar.copy(dst, src[:, :, :, 2:4])
+            dst = stage[g][:, :, lo // PACK : hi // PACK, :].rearrange("p t m j -> p m j t")
+            nc.vector.tensor_copy(dst[:, :, :, 0:share], src[:, :, :, 0:share])
+            nc.scalar.copy(dst[:, :, :, share:PACK], src[:, :, :, share:PACK])
             if hi == H:
-                for u in range(2):
-                    cols = slice(2 * P * u, 2 * P * (u + 1))
+                step = 2 - g
+                for t in range(0, PACK, step):
+                    cols = slice(P * t, P * (t + step))
                     nc.vector.quantize_mx(
                         out=w1q[g][:, cols].bitcast(FP8X4),
                         scales=w1s[g][:, cols],
-                        in_=stage[g][u][:].rearrange("p t m j -> p (t m j)"),
+                        in_=stage[g][:, t : t + step].rearrange("p t m j -> p (t m j)"),
                     )
 
         old0 = sb("old0", [P, S], F32)
@@ -215,9 +216,9 @@ def tile_picked_modres_mlpgelu_p_kernel(
         layer1(1)
         gy0 = layer2(0, CHUNK)
         layer1(2)
+        fetch_old1(0, "h2")
         layer2_turned(1)
         layer1(3)
-        fetch_old1(0, "h3")
         layer2_turned(2)
         layer2_turned(3)
         for b in range(2):

@@ -3,12 +3,15 @@ from contextlib import ExitStack
 import concourse.mybir as mybir
 
 K, T, S, H, N = 1024, 1024, 512, 512, 256
+FLOPS = 2 * S * (K * H + H * N)
+
 P = 128
 PACK = 4
 PASSES = K // (P * PACK)
+QUADRANTS = 4
+BLOCKS = N // P
 CHUNK = 128
 HALF = S // 2
-FLOPS = 2 * S * (K * H + H * N)
 
 F32 = mybir.dt.float32
 BF16 = mybir.dt.bfloat16
@@ -24,6 +27,11 @@ IS_EQUAL = mybir.AluOpType.is_equal
 ADD = mybir.AluOpType.add
 MULT = mybir.AluOpType.mult
 
+W1_PIECE_AT = (0, 8192, 12288)
+X_SCALES_AT = 16768
+
+W1_PIECES = ((0, 0, H, 2), (1, 0, H // 2, 1), (1, H // 2, H, 2))
+
 
 def tile_picked_modres_mlpgelu_p_kernel(
     tc, x_words, x_scales, gate, res, w1, w2_words, w2_scales, offs, out
@@ -31,200 +39,192 @@ def tile_picked_modres_mlpgelu_p_kernel(
     nc = tc.nc
     with ExitStack() as ctx:
         keep = ctx.enter_context(tc.tile_pool(name="keep", bufs=1))
-        stream = ctx.enter_context(tc.tile_pool(name="stream", bufs=1))
+        by_hand = ctx.enter_context(tc.tile_pool(name="by_hand", bufs=1))
         psum = ctx.enter_context(tc.psum_pool(name="psum", bufs=1))
 
-        def sb(name, shape, dtype, tag=None):
-            return keep.tile(shape, dtype, name=name, tag=tag or name, align_bytes=64)
+        def sbuf(name, shape, dtype, reuses=None):
+            return keep.tile(shape, dtype, name=name, tag=reuses or name, align_bytes=64)
 
         def placed(name, shape, dtype, offset):
-            return stream.tile(shape, dtype, name=name, offset=offset, align_bytes=64)
+            return by_hand.tile(shape, dtype, name=name, offset=offset, align_bytes=64)
 
-        offsets = sb("offsets", [P, S // 16], U16)
+        offsets = sbuf("offsets", [P, S // 16], U16)
         nc.sync.dma_start(offsets[:], offs)
 
         def entries(lo, hi):
             return offsets[:, lo // 16 : hi // 16]
 
-        xs_all = placed("xs_all", [P, T], U8, 16768)
-        nc.gpsimd.memset(xs_all[:].bitcast(I32), 0)
-        ones = sb("ones", [P, P], F32)
+        x_scale_window = placed("x_scale_window", [P, T], U8, X_SCALES_AT)
+        nc.gpsimd.memset(x_scale_window[:].bitcast(I32), 0)
+        ones = sbuf("ones", [P, P], F32)
         nc.vector.memset(ones[:], 1.0)
-        ident = sb("ident", [P, P], F32)
+        identity = sbuf("identity", [P, P], F32)
         nc.gpsimd.affine_select(
-            out=ident[:], in_=ones[:], compare_op=IS_EQUAL, fill=0.0, base=0, pattern=[[-1, P]], channel_multiplier=1
+            out=identity[:], in_=ones[:], compare_op=IS_EQUAL, fill=0.0, base=0, pattern=[[-1, P]], channel_multiplier=1
         )
-        w2s = sb("w2s", [P, N], U8, "ones")
-        nc.gpsimd.memset(w2s[:].bitcast(I32), 0)
-        warm_in = placed("warm_in", [P, 32], F32, 8192 - 64)
-        warm_out = placed("warm_out", [P, 16], F32, 12288)
-        nc.vector.memset(warm_in[:], 0.0)
-        nc.scalar.activation(warm_out[:], warm_in[:, 0:16], GELU)
+        w2_scale = sbuf("w2_scale", [P, N], U8, reuses="ones")
+        nc.gpsimd.memset(w2_scale[:].bitcast(I32), 0)
 
-        xw_all = []
+        table_in = placed("table_in", [P, 32], F32, W1_PIECE_AT[1] - 64)
+        table_out = placed("table_out", [P, 16], F32, W1_PIECE_AT[2])
+        nc.vector.memset(table_in[:], 0.0)
+        nc.scalar.activation(table_out[:], table_in[:, 0:16], GELU)
+
+        x_word_window = []
         for g in range(PASSES):
-            t = sb("xw_all%d" % g, [P, T], U32)
-            nc.sync.dma_start(t[:].bitcast(I32), x_words[g].rearrange("p n t -> p (n t)").bitcast(I32))
-            xw_all.append(t)
-        for q in range(4):
+            window = sbuf("x_word_window%d" % g, [P, T], U32)
+            nc.sync.dma_start(window[:].bitcast(I32), x_words[g].rearrange("p n j -> p (n j)").bitcast(I32))
+            x_word_window.append(window)
+        for q in range(QUADRANTS):
             nc.sync.dma_start(
-                xs_all[32 * q : 32 * q + 8, :].bitcast(I32),
+                x_scale_window[32 * q : 32 * q + 4 * PASSES, :].bitcast(I32),
                 x_scales[:, 4 * q : 4 * q + 4, :].bitcast(I32),
             )
-        for q in range(4):
+        for q in range(QUADRANTS):
             nc.gpsimd.dma_start(
-                w2s[32 * q : 32 * q + 4, :].bitcast(I32),
+                w2_scale[32 * q : 32 * q + 4, :].bitcast(I32),
                 w2_scales[0][4 * q : 4 * q + 4, :].bitcast(I32),
             )
 
         w1_rows = w1.rearrange("(g p j) c -> g p j c", g=PASSES, j=PACK)
-        pieces = [(0, 0, H, 0, 2), (1, 0, H // 2, 8192, 1), (1, H // 2, H, 12288, 2)]
-        raw = []
-        for i, (g, lo, hi, at, share) in enumerate(pieces):
-            t = placed("w1_raw%d" % i, [P, PACK, hi - lo], F32, at)
-            nc.sync.dma_start(t[:], w1_rows[g][:, :, lo:hi])
-            raw.append(t)
+        w1_raw = []
+        for i, (g, lo, hi, on_vector) in enumerate(W1_PIECES):
+            piece = placed("w1_raw%d" % i, [P, PACK, hi - lo], F32, W1_PIECE_AT[i])
+            nc.sync.dma_start(piece[:], w1_rows[g][:, :, lo:hi])
+            w1_raw.append(piece)
 
-        xw = [sb("xw%d" % g, [P, S], U32) for g in range(PASSES)]
+        x_word = [sbuf("x_word%d" % g, [P, S], U32) for g in range(PASSES)]
         for g in range(PASSES):
-            nc.vector.tensor_copy(xw[g][:], xw_all[g][:].indirect(offsets[:]))
-        xs = sb("xs", [P, S], U8)
-        nc.vector.tensor_copy(xs[:], xs_all[:].indirect(offsets[:]))
+            nc.vector.tensor_copy(x_word[g][:], x_word_window[g][:].indirect(offsets[:]))
+        x_scale = sbuf("x_scale", [P, S], U8)
+        nc.vector.tensor_copy(x_scale[:], x_scale_window[:].indirect(offsets[:]))
 
-        rows = [sb("rows%d" % b, [P, T], F32, "xw_all%d" % b) for b in range(2)]
-        for b in range(2):
+        rows = [sbuf("rows%d" % b, [P, T], F32, reuses="x_word_window%d" % b) for b in range(BLOCKS)]
+        for b in range(BLOCKS):
             nc.sync.dma_start(rows[b][:], res[P * b : P * (b + 1), :])
-        w2w = placed("w2w", [P, 2 * N], U8, 16768)
-        nc.sync.dma_start(w2w[:].bitcast(I32), w2_words[0].bitcast(I32))
-        gate_col = placed("gate_col", [P, S // P - 1], F32, 16768 + 512)
-        gate_sb = placed("gate_sb", [P, CHUNK], F32, 16768 + 576)
-        nc.sync.dma_start(gate_sb[:], gate[:, 0:CHUNK])
+        w2_word = placed("w2_word", [P, 2 * N], U8, X_SCALES_AT)
+        nc.sync.dma_start(w2_word[:].bitcast(I32), w2_words[0].bitcast(I32))
+        gate_by_partition = placed("gate_by_partition", [P, S // CHUNK - 1], F32, X_SCALES_AT + 2 * N)
+        gate_first = placed("gate_first", [P, CHUNK], F32, X_SCALES_AT + 2 * N + 64)
+        nc.sync.dma_start(gate_first[:], gate[:, 0:CHUNK])
         with nc.allow_non_contiguous_dma(reason="one gate value a partition"):
-            nc.sync.dma_start(gate_col[:], gate[0, CHUNK:S].rearrange("(c p) -> p c", p=P))
+            nc.sync.dma_start(gate_by_partition[:], gate[0, CHUNK:S].rearrange("(c p) -> p c", p=P))
 
-        stage = [sb("stage%d" % g, [P, PACK, P, PACK], BF16) for g in range(PASSES)]
-        w1q = [sb("w1q%d" % g, [P, H], U32) for g in range(PASSES)]
-        w1s = [sb("w1s%d" % g, [P, H], U8) for g in range(PASSES)]
-        for i, (g, lo, hi, at, share) in enumerate(pieces):
-            src = raw[i][:].rearrange("p j (m t) -> p m j t", t=PACK)
-            dst = stage[g][:, :, lo // PACK : hi // PACK, :].rearrange("p t m j -> p m j t")
-            nc.vector.tensor_copy(dst[:, :, :, 0:share], src[:, :, :, 0:share])
-            nc.scalar.copy(dst[:, :, :, share:PACK], src[:, :, :, share:PACK])
+        w1_bf16 = [sbuf("w1_bf16_%d" % g, [P, PACK, P, PACK], BF16) for g in range(PASSES)]
+        w1_word = [sbuf("w1_word%d" % g, [P, H], U32) for g in range(PASSES)]
+        w1_scale = [sbuf("w1_scale%d" % g, [P, H], U8) for g in range(PASSES)]
+        for i, (g, lo, hi, on_vector) in enumerate(W1_PIECES):
+            src = w1_raw[i][:].rearrange("p j (m t) -> p m j t", t=PACK)
+            dst = w1_bf16[g][:, :, lo // PACK : hi // PACK, :].rearrange("p t m j -> p m j t")
+            nc.vector.tensor_copy(dst[:, :, :, 0:on_vector], src[:, :, :, 0:on_vector])
+            nc.scalar.copy(dst[:, :, :, on_vector:PACK], src[:, :, :, on_vector:PACK])
             if hi == H:
-                step = 2 - g
-                for t in range(0, PACK, step):
-                    cols = slice(P * t, P * (t + step))
+                tiles_a_call = 1 if g == PASSES - 1 else 2
+                for t in range(0, PACK, tiles_a_call):
+                    cols = slice(P * t, P * (t + tiles_a_call))
                     nc.vector.quantize_mx(
-                        out=w1q[g][:, cols].bitcast(FP8X4),
-                        scales=w1s[g][:, cols],
-                        in_=stage[g][:, t : t + step].rearrange("p t m j -> p (t m j)"),
+                        out=w1_word[g][:, cols].bitcast(FP8X4),
+                        scales=w1_scale[g][:, cols],
+                        in_=w1_bf16[g][:, t : t + tiles_a_call].rearrange("p t m j -> p (t m j)"),
                     )
 
-        old0 = sb("old0", [P, S], F32)
-        old1 = {}
-        hq = sb("hq", [P, S], U32)
-        hs = sb("hs", [P, S], U8)
+        h_word = sbuf("h_word", [P, S], U32)
+        h_scale = sbuf("h_scale", [P, S], U8)
 
-        def layer1(c):
+        def first_layer(c):
             cols = slice(CHUNK * c, CHUNK * (c + 1))
             acc = psum.tile([P, PACK, CHUNK], F32, name="acc%d" % c)
             for t in range(PACK):
-                m = slice(P * t, P * (t + 1))
+                units = slice(P * t, P * (t + 1))
                 for g in range(PASSES):
                     nc.tensor.matmul_mx(
                         out=acc[:, t, :],
-                        lhsT=w1q[g][:, m].bitcast(FP8X4),
-                        lhsT_scale=w1s[g][:, m],
-                        rhs=xw[g][:, cols].bitcast(FP8X4),
-                        rhs_scale=xs[4 * g : P, cols],
+                        lhsT=w1_word[g][:, units].bitcast(FP8X4),
+                        lhsT_scale=w1_scale[g][:, units],
+                        rhs=x_word[g][:, cols].bitcast(FP8X4),
+                        rhs_scale=x_scale[4 * g : P, cols],
                         start=(g == 0),
                         stop=(g == PASSES - 1),
                     )
-            h = sb("h%d" % c, [P, CHUNK, PACK], BF16)
+            h = sbuf("h%d" % c, [P, CHUNK, PACK], BF16)
             nc.scalar.activation(h[:], acc[:].rearrange("p t n -> p n t"), GELU)
             nc.vector.quantize_mx(
-                out=hq[:, cols].bitcast(FP8X4), scales=hs[:, cols], in_=h[:].rearrange("p n t -> p (n t)")
+                out=h_word[:, cols].bitcast(FP8X4), scales=h_scale[:, cols], in_=h[:].rearrange("p n t -> p (n t)")
             )
 
-        def layer2(lo, hi):
-            y = psum.tile([P, 2, hi - lo], F32, name="y%d" % lo, tag="y", bufs=2)
-            for b in range(2):
-                for c0 in range(lo, hi, CHUNK):
-                    nc.tensor.matmul_mx(
-                        out=y[:, b, c0 - lo : c0 - lo + CHUNK],
-                        lhsT=w2w[:, 2 * P * b : 2 * P * (b + 1)].bitcast(FP4X4),
-                        lhsT_scale=w2s[:, P * b : P * (b + 1)],
-                        rhs=hq[:, c0 : c0 + CHUNK].bitcast(FP8X4),
-                        rhs_scale=hs[:, c0 : c0 + CHUNK],
-                        start=True,
-                        stop=True,
-                    )
-            gy = sb("gy%d" % lo, [P, 2, hi - lo], F32)
-            nc.vector.tensor_tensor(
-                gy[:], y[:], gate_sb[:, lo:hi].unsqueeze(1).to_broadcast([P, 2, hi - lo]), MULT
-            )
-            return gy
+        def second_layer_first_chunk():
+            y = psum.tile([P, BLOCKS, CHUNK], F32, name="y0", tag="y", bufs=2)
+            for b in range(BLOCKS):
+                nc.tensor.matmul_mx(
+                    out=y[:, b, :],
+                    lhsT=w2_word[:, 2 * P * b : 2 * P * (b + 1)].bitcast(FP4X4),
+                    lhsT_scale=w2_scale[:, P * b : P * (b + 1)],
+                    rhs=h_word[:, 0:CHUNK].bitcast(FP8X4),
+                    rhs_scale=h_scale[:, 0:CHUNK],
+                    start=True,
+                    stop=True,
+                )
+            gated = sbuf("gated_first", [P, BLOCKS, CHUNK], F32)
+            nc.vector.tensor_tensor(gated[:], y[:], gate_first[:].unsqueeze(1).to_broadcast([P, BLOCKS, CHUNK]), MULT)
+            return gated
 
-        gy_late = sb("gy_late", [P, 2, S - CHUNK], F32)
+        gated_rest = sbuf("gated_rest", [P, BLOCKS, S - CHUNK], F32)
 
-        def layer2_turned(c):
+        def second_layer_turned(c):
             cols = slice(CHUNK * c, CHUNK * (c + 1))
-            yt = psum.tile([P, N], F32, name="yt%d" % c, tag="y", bufs=2)
+            y_turned = psum.tile([P, N], F32, name="y%d" % c, tag="y", bufs=2)
             nc.tensor.matmul_mx(
-                out=yt[:],
-                lhsT=hq[:, cols].bitcast(FP8X4),
-                lhsT_scale=hs[:, cols],
-                rhs=w2w[:].bitcast(FP4X4),
-                rhs_scale=w2s[:],
+                out=y_turned[:],
+                lhsT=h_word[:, cols].bitcast(FP8X4),
+                lhsT_scale=h_scale[:, cols],
+                rhs=w2_word[:].bitcast(FP4X4),
+                rhs_scale=w2_scale[:],
                 start=True,
                 stop=True,
             )
-            gyt = sb("gyt%d" % c, [P, N], F32)
-            nc.scalar.activation(gyt[:], yt[:], COPY, scale=gate_col[:, c - 1 : c])
-            back = psum.tile([P, 2, CHUNK], F32, name="back%d" % c, tag="back", bufs=2)
-            for b in range(2):
-                nc.tensor.transpose(back[:, b, :], gyt[:, P * b : P * (b + 1)], ident[:])
-            nc.scalar.copy(gy_late[:, :, CHUNK * (c - 1) : CHUNK * c], back[:])
+            gated_turned = sbuf("gated_turned%d" % c, [P, N], F32)
+            nc.scalar.activation(gated_turned[:], y_turned[:], COPY, scale=gate_by_partition[:, c - 1 : c])
+            back = psum.tile([P, BLOCKS, CHUNK], F32, name="back%d" % c, tag="back", bufs=2)
+            for b in range(BLOCKS):
+                nc.tensor.transpose(back[:, b, :], gated_turned[:, P * b : P * (b + 1)], identity[:])
+            nc.scalar.copy(gated_rest[:, :, CHUNK * (c - 1) : CHUNK * c], back[:])
 
-        def old_cols(b, lo, hi):
-            if b == 0:
-                return old0[:, lo:hi]
-            base = lo // HALF * HALF
-            return old1[base][:, lo - base : hi - base]
+        def look_up_res(name, b, lo, hi, reuses=None):
+            old = sbuf(name, [P, hi - lo], F32, reuses)
+            nc.vector.tensor_copy(old[:], rows[b][:].indirect(entries(lo, hi)))
+            return old
 
-        def fetch_old1(base, tag):
-            old1[base] = sb("old1_%d" % base, [P, HALF], F32, tag)
-            nc.vector.tensor_copy(old1[base][:], rows[1][:].indirect(entries(base, base + HALF)))
-
-        def put(vals, lo, hi, b):
-            nc.vector.tensor_tensor(rows[b][:].indirect(entries(lo, hi)), vals, old_cols(b, lo, hi), ADD)
+        def put_back(b, lo, hi, gated, old):
+            nc.vector.tensor_tensor(rows[b][:].indirect(entries(lo, hi)), gated, old, ADD)
 
         for i in range(2):
-            warm_acc = psum.tile([P, S], F32, name="warm_acc%d" % i, tag="back", bufs=2)
+            warm_up = psum.tile([P, S], F32, name="warm_up%d" % i, tag="back", bufs=2)
             nc.tensor.matmul_mx(
-                out=warm_acc[:],
-                lhsT=w1q[0][:, 0:P].bitcast(FP8X4),
-                lhsT_scale=w1s[0][:, 0:P],
-                rhs=xw[0][:].bitcast(FP8X4),
-                rhs_scale=xs[:],
+                out=warm_up[:],
+                lhsT=w1_word[0][:, 0:P].bitcast(FP8X4),
+                lhsT_scale=w1_scale[0][:, 0:P],
+                rhs=x_word[0][:].bitcast(FP8X4),
+                rhs_scale=x_scale[:],
                 start=True,
                 stop=True,
             )
-        nc.vector.tensor_copy(old0[:], rows[0][:].indirect(offsets[:]))
-        layer1(0)
-        fetch_old1(HALF, "h0")
-        layer1(1)
-        gy0 = layer2(0, CHUNK)
-        layer1(2)
-        fetch_old1(0, "h2")
-        layer2_turned(1)
-        layer1(3)
-        layer2_turned(2)
-        layer2_turned(3)
-        for b in range(2):
-            put(gy0[:, b, :], 0, CHUNK, b)
-        put(gy_late[:, 0, 0:CHUNK], CHUNK, 2 * CHUNK, 0)
-        put(gy_late[:, 1, 0:CHUNK], CHUNK, 2 * CHUNK, 1)
-        for b in range(2):
-            put(gy_late[:, b, CHUNK:], 2 * CHUNK, S, b)
+
+        old0 = look_up_res("old0", 0, 0, S)
+        first_layer(0)
+        old1_high = look_up_res("old1_high", 1, HALF, S, reuses="h0")
+        first_layer(1)
+        gated_first = second_layer_first_chunk()
+        first_layer(2)
+        second_layer_turned(1)
+        first_layer(3)
+        old1_low = look_up_res("old1_low", 1, 0, HALF, reuses="h3")
+        second_layer_turned(2)
+        second_layer_turned(3)
+
+        put_back(0, 0, CHUNK, gated_first[:, 0, :], old0[:, 0:CHUNK])
+        put_back(1, 0, CHUNK, gated_first[:, 1, :], old1_low[:, 0:CHUNK])
+        put_back(0, CHUNK, HALF, gated_rest[:, 0, 0:CHUNK], old0[:, CHUNK:HALF])
+        put_back(1, CHUNK, HALF, gated_rest[:, 1, 0:CHUNK], old1_low[:, CHUNK:HALF])
+        for b, old in ((0, old0[:, HALF:S]), (1, old1_high[:])):
+            put_back(b, HALF, S, gated_rest[:, b, CHUNK:], old)
             nc.sync.dma_start(out[P * b : P * (b + 1), :], rows[b][:])

@@ -27,10 +27,11 @@ IS_EQUAL = mybir.AluOpType.is_equal
 ADD = mybir.AluOpType.add
 MULT = mybir.AluOpType.mult
 
-W1_PIECE_AT = (0, 8192, 12288)
+W1_PIECE_BYTES = 4096
 X_SCALES_AT = 16768
+SHARED_AT = 18432
 
-W1_PIECES = ((0, 0, H, 2), (1, 0, H // 2, 1), (1, H // 2, H, 2))
+W1_PIECES = ((0, 0, H // 2, 0), (0, H // 2, H, 2), (1, 0, H // 2, 2), (1, H // 2, H, 2))
 
 
 def tile_picked_modres_mlpgelu_p_kernel(
@@ -48,48 +49,46 @@ def tile_picked_modres_mlpgelu_p_kernel(
         def placed(name, shape, dtype, offset):
             return by_hand.tile(shape, dtype, name=name, offset=offset, align_bytes=64)
 
+        x_scale_window = placed("x_scale_window", [P, T], U8, X_SCALES_AT)
+        nc.gpsimd.memset(x_scale_window[:].bitcast(I32), 0)
+        w2_scale = sbuf("w2_scale", [P, N], U8)
+        nc.vector.memset(w2_scale[:].bitcast(I32), 0)
+
+        table_in = sbuf("table_in", [P, 16], F32)
+        table_out = sbuf("table_out", [P, 16], F32)
+        nc.vector.memset(table_in[:], 0.0)
+        nc.scalar.activation(table_out[:], table_in[:], GELU)
+
         offsets = sbuf("offsets", [P, S // 16], U16)
-        nc.sync.dma_start(offsets[:], offs)
 
         def entries(lo, hi):
             return offsets[:, lo // 16 : hi // 16]
-
-        x_scale_window = placed("x_scale_window", [P, T], U8, X_SCALES_AT)
-        nc.gpsimd.memset(x_scale_window[:].bitcast(I32), 0)
-        ones = sbuf("ones", [P, P], F32)
-        nc.vector.memset(ones[:], 1.0)
-        identity = sbuf("identity", [P, P], F32)
-        nc.gpsimd.affine_select(
-            out=identity[:], in_=ones[:], compare_op=IS_EQUAL, fill=0.0, base=0, pattern=[[-1, P]], channel_multiplier=1
-        )
-        w2_scale = sbuf("w2_scale", [P, N], U8, reuses="ones")
-        nc.gpsimd.memset(w2_scale[:].bitcast(I32), 0)
-
-        table_in = placed("table_in", [P, 32], F32, W1_PIECE_AT[1] - 64)
-        table_out = placed("table_out", [P, 16], F32, W1_PIECE_AT[2])
-        nc.vector.memset(table_in[:], 0.0)
-        nc.scalar.activation(table_out[:], table_in[:, 0:16], GELU)
 
         x_word_window = []
         for g in range(PASSES):
             window = sbuf("x_word_window%d" % g, [P, T], U32)
             nc.sync.dma_start(window[:].bitcast(I32), x_words[g].rearrange("p n j -> p (n j)").bitcast(I32))
             x_word_window.append(window)
+            if g == 0:
+                nc.sync.dma_start(offsets[:], offs)
         for q in range(QUADRANTS):
-            nc.sync.dma_start(
+            nc.scalar.dma_start(
                 x_scale_window[32 * q : 32 * q + 4 * PASSES, :].bitcast(I32),
                 x_scales[:, 4 * q : 4 * q + 4, :].bitcast(I32),
             )
-        for q in range(QUADRANTS):
-            nc.gpsimd.dma_start(
-                w2_scale[32 * q : 32 * q + 4, :].bitcast(I32),
-                w2_scales[0][4 * q : 4 * q + 4, :].bitcast(I32),
-            )
+        ones = sbuf("ones", [P, P], F32)
+        nc.vector.memset(ones[:], 1.0)
+        identity = sbuf("identity", [P, P], F32)
+        nc.gpsimd.affine_select(
+            out=identity[:], in_=ones[:], compare_op=IS_EQUAL, fill=0.0, base=0, pattern=[[-1, P]], channel_multiplier=1
+        )
 
         w1_rows = w1.rearrange("(g p j) c -> g p j c", g=PASSES, j=PACK)
         w1_raw = []
+        at = 0
         for i, (g, lo, hi, on_vector) in enumerate(W1_PIECES):
-            piece = placed("w1_raw%d" % i, [P, PACK, hi - lo], F32, W1_PIECE_AT[i])
+            piece = placed("w1_raw%d" % i, [P, PACK, hi - lo], F32, at)
+            at = at + 4 * PACK * (hi - lo)
             nc.sync.dma_start(piece[:], w1_rows[g][:, :, lo:hi])
             w1_raw.append(piece)
 
@@ -99,37 +98,44 @@ def tile_picked_modres_mlpgelu_p_kernel(
         x_scale = sbuf("x_scale", [P, S], U8)
         nc.vector.tensor_copy(x_scale[:], x_scale_window[:].indirect(offsets[:]))
 
-        rows = [sbuf("rows%d" % b, [P, T], F32, reuses="x_word_window%d" % b) for b in range(BLOCKS)]
+        rows = [sbuf("rows%d" % b, [P, T], F32) for b in range(BLOCKS)]
         for b in range(BLOCKS):
             nc.sync.dma_start(rows[b][:], res[P * b : P * (b + 1), :])
-        w2_word = placed("w2_word", [P, 2 * N], U8, X_SCALES_AT)
+        w2_word = sbuf("w2_word", [P, 2 * N], U8)
         nc.sync.dma_start(w2_word[:].bitcast(I32), w2_words[0].bitcast(I32))
-        gate_by_partition = placed("gate_by_partition", [P, S // CHUNK - 1], F32, X_SCALES_AT + 2 * N)
-        gate_first = placed("gate_first", [P, CHUNK], F32, X_SCALES_AT + 2 * N + 64)
+        gate_first = sbuf("gate_first", [P, CHUNK], F32)
         nc.sync.dma_start(gate_first[:], gate[:, 0:CHUNK])
+        for q in range(QUADRANTS):
+            nc.sync.dma_start(
+                w2_scale[32 * q : 32 * q + 4, :].bitcast(I32),
+                w2_scales[0][4 * q : 4 * q + 4, :].bitcast(I32),
+            )
+        gate_by_partition = sbuf("gate_by_partition", [P, S // CHUNK - 1], F32)
         with nc.allow_non_contiguous_dma(reason="one gate value a partition"):
             nc.sync.dma_start(gate_by_partition[:], gate[0, CHUNK:S].rearrange("(c p) -> p c", p=P))
 
-        w1_bf16 = [sbuf("w1_bf16_%d" % g, [P, PACK, P, PACK], BF16) for g in range(PASSES)]
         w1_word = [sbuf("w1_word%d" % g, [P, H], U32) for g in range(PASSES)]
         w1_scale = [sbuf("w1_scale%d" % g, [P, H], U8) for g in range(PASSES)]
         for i, (g, lo, hi, on_vector) in enumerate(W1_PIECES):
+            width = (hi - lo) // PACK
+            rounded = sbuf("w1_bf16_%d" % i, [P, PACK, width, PACK], BF16)
             src = w1_raw[i][:].rearrange("p j (m t) -> p m j t", t=PACK)
-            dst = w1_bf16[g][:, :, lo // PACK : hi // PACK, :].rearrange("p t m j -> p m j t")
-            nc.vector.tensor_copy(dst[:, :, :, 0:on_vector], src[:, :, :, 0:on_vector])
-            nc.scalar.copy(dst[:, :, :, on_vector:PACK], src[:, :, :, on_vector:PACK])
-            if hi == H:
-                tiles_a_call = 1 if g == PASSES - 1 else 2
-                for t in range(0, PACK, tiles_a_call):
-                    cols = slice(P * t, P * (t + tiles_a_call))
-                    nc.vector.quantize_mx(
-                        out=w1_word[g][:, cols].bitcast(FP8X4),
-                        scales=w1_scale[g][:, cols],
-                        in_=w1_bf16[g][:, t : t + tiles_a_call].rearrange("p t m j -> p (t m j)"),
-                    )
+            dst = rounded[:].rearrange("p t m j -> p m j t")
+            if on_vector > 0:
+                nc.vector.tensor_copy(dst[:, :, :, 0:on_vector], src[:, :, :, 0:on_vector])
+            if on_vector < PACK:
+                nc.scalar.copy(dst[:, :, :, on_vector:PACK], src[:, :, :, on_vector:PACK])
+            tiles_a_call = 2 if width == P else 1
+            for t in range(0, PACK, tiles_a_call):
+                cols = slice(P * t + lo // PACK, P * (t + tiles_a_call - 1) + hi // PACK)
+                nc.vector.quantize_mx(
+                    out=w1_word[g][:, cols].bitcast(FP8X4),
+                    scales=w1_scale[g][:, cols],
+                    in_=rounded[:, t : t + tiles_a_call].rearrange("p t m j -> p (t m j)"),
+                )
 
-        h_word = sbuf("h_word", [P, S], U32)
-        h_scale = sbuf("h_scale", [P, S], U8)
+        h_word = {}
+        h_scale = [sbuf("h_scale%d" % c, [P, CHUNK], U8) for c in range(S // CHUNK)]
 
         def first_layer(c):
             cols = slice(CHUNK * c, CHUNK * (c + 1))
@@ -146,10 +152,17 @@ def tile_picked_modres_mlpgelu_p_kernel(
                         start=(g == 0),
                         stop=(g == PASSES - 1),
                     )
-            h = sbuf("h%d" % c, [P, CHUNK, PACK], BF16)
+            if c == 1:
+                h = placed("h%d" % c, [P, CHUNK, PACK], BF16, SHARED_AT)
+            else:
+                h = sbuf("h%d" % c, [P, CHUNK, PACK], BF16)
+            if c == 9:
+                h_word[c] = placed("h_word%d" % c, [P, CHUNK], U32, SHARED_AT)
+            else:
+                h_word[c] = sbuf("h_word%d" % c, [P, CHUNK], U32)
             nc.scalar.activation(h[:], acc[:].rearrange("p t n -> p n t"), GELU)
             nc.vector.quantize_mx(
-                out=h_word[:, cols].bitcast(FP8X4), scales=h_scale[:, cols], in_=h[:].rearrange("p n t -> p (n t)")
+                out=h_word[c][:].bitcast(FP8X4), scales=h_scale[c][:], in_=h[:].rearrange("p n t -> p (n t)")
             )
 
         def second_layer_first_chunk():
@@ -159,24 +172,24 @@ def tile_picked_modres_mlpgelu_p_kernel(
                     out=y[:, b, :],
                     lhsT=w2_word[:, 2 * P * b : 2 * P * (b + 1)].bitcast(FP4X4),
                     lhsT_scale=w2_scale[:, P * b : P * (b + 1)],
-                    rhs=h_word[:, 0:CHUNK].bitcast(FP8X4),
-                    rhs_scale=h_scale[:, 0:CHUNK],
+                    rhs=h_word[0][:].bitcast(FP8X4),
+                    rhs_scale=h_scale[0][:],
                     start=True,
                     stop=True,
                 )
-            gated = sbuf("gated_first", [P, BLOCKS, CHUNK], F32)
-            nc.vector.tensor_tensor(gated[:], y[:], gate_first[:].unsqueeze(1).to_broadcast([P, BLOCKS, CHUNK]), MULT)
+            gated = [placed("gated_first%d" % b, [P, CHUNK], F32, SHARED_AT + 4 * CHUNK * b) for b in range(BLOCKS)]
+            for b in range(BLOCKS):
+                nc.vector.tensor_tensor(gated[b][:], y[:, b, :], gate_first[:], MULT)
             return gated
 
         gated_rest = sbuf("gated_rest", [P, BLOCKS, S - CHUNK], F32)
 
         def second_layer_turned(c):
-            cols = slice(CHUNK * c, CHUNK * (c + 1))
             y_turned = psum.tile([P, N], F32, name="y%d" % c, tag="y", bufs=2)
             nc.tensor.matmul_mx(
                 out=y_turned[:],
-                lhsT=h_word[:, cols].bitcast(FP8X4),
-                lhsT_scale=h_scale[:, cols],
+                lhsT=h_word[c][:].bitcast(FP8X4),
+                lhsT_scale=h_scale[c][:],
                 rhs=w2_word[:].bitcast(FP4X4),
                 rhs_scale=w2_scale[:],
                 start=True,
@@ -197,34 +210,34 @@ def tile_picked_modres_mlpgelu_p_kernel(
         def put_back(b, lo, hi, gated, old):
             nc.vector.tensor_tensor(rows[b][:].indirect(entries(lo, hi)), gated, old, ADD)
 
-        for i in range(2):
-            warm_up = psum.tile([P, S], F32, name="warm_up%d" % i, tag="back", bufs=2)
+        for i, width in enumerate((512, 512, 256)):
+            warm_up = psum.tile([P, width], F32, name="warm_up%d" % i, tag="back", bufs=2)
             nc.tensor.matmul_mx(
                 out=warm_up[:],
-                lhsT=w1_word[0][:, 0:P].bitcast(FP8X4),
-                lhsT_scale=w1_scale[0][:, 0:P],
-                rhs=x_word[0][:].bitcast(FP8X4),
-                rhs_scale=x_scale[:],
+                lhsT=x_word[0][:, 0:P].bitcast(FP8X4),
+                lhsT_scale=x_scale[:, 0:P],
+                rhs=x_word[0][:, 0:width].bitcast(FP8X4),
+                rhs_scale=x_scale[:, 0:width],
                 start=True,
                 stop=True,
             )
 
         old0 = look_up_res("old0", 0, 0, S)
+        old1 = look_up_res("old1", 1, 0, S)
+        old = (old0, old1)
         first_layer(0)
-        old1_high = look_up_res("old1_high", 1, HALF, S, reuses="h0")
         first_layer(1)
         gated_first = second_layer_first_chunk()
         first_layer(2)
         second_layer_turned(1)
+        for b in range(BLOCKS):
+            put_back(b, 0, CHUNK, gated_first[b][:], old[b][:, 0:CHUNK])
         first_layer(3)
-        old1_low = look_up_res("old1_low", 1, 0, HALF, reuses="h3")
         second_layer_turned(2)
         second_layer_turned(3)
 
-        put_back(0, 0, CHUNK, gated_first[:, 0, :], old0[:, 0:CHUNK])
-        put_back(1, 0, CHUNK, gated_first[:, 1, :], old1_low[:, 0:CHUNK])
-        put_back(0, CHUNK, HALF, gated_rest[:, 0, 0:CHUNK], old0[:, CHUNK:HALF])
-        put_back(1, CHUNK, HALF, gated_rest[:, 1, 0:CHUNK], old1_low[:, CHUNK:HALF])
-        for b, old in ((0, old0[:, HALF:S]), (1, old1_high[:])):
-            put_back(b, HALF, S, gated_rest[:, b, CHUNK:], old)
-            nc.sync.dma_start(out[P * b : P * (b + 1), :], rows[b][:])
+        for lo, hi in ((CHUNK, HALF), (HALF, S)):
+            for b in range(BLOCKS):
+                put_back(b, lo, hi, gated_rest[:, b, lo - CHUNK : hi - CHUNK], old[b][:, lo:hi])
+                if hi == S:
+                    nc.sync.dma_start(out[P * b : P * (b + 1), :], rows[b][:])

@@ -1,6 +1,7 @@
 from contextlib import ExitStack
 
 import concourse.mybir as mybir
+from concourse.masks import make_identity
 
 K, T, S, H, N = 1024, 1024, 512, 512, 256
 FLOPS = 2 * S * (K * H + H * N)
@@ -11,6 +12,7 @@ PASSES = K // (P * PACK)
 QUADRANTS = 4
 BLOCKS = N // P
 CHUNK = 128
+CHUNKS = S // CHUNK
 HALF = S // 2
 
 F32 = mybir.dt.float32
@@ -23,15 +25,15 @@ FP8X4 = mybir.dt.float8_e4m3fn_x4
 FP4X4 = mybir.dt.float4_e2m1fn_x4
 GELU = mybir.ActivationFunctionType.Gelu_apprx_tanh
 COPY = mybir.ActivationFunctionType.Copy
-IS_EQUAL = mybir.AluOpType.is_equal
 ADD = mybir.AluOpType.add
 MULT = mybir.AluOpType.mult
 
-W1_PIECE_BYTES = 4096
-X_SCALES_AT = 16768
-SHARED_AT = 18432
-
-W1_PIECES = ((0, 0, H // 2, 0), (0, H // 2, H, 2), (1, 0, H // 2, 2), (1, H // 2, H, 2))
+EXTRA_ON_VECTOR = (0, 32)
+HOLD_CHUNK = 3
+X_WORDS_AT = 1024
+X_SCALES_AT = X_WORDS_AT + 8 * T
+W1_AT = X_SCALES_AT + T
+ROUNDED_AT = W1_AT + 4 * PASSES * PACK * H
 
 
 def tile_picked_modres_mlpgelu_p_kernel(
@@ -43,149 +45,161 @@ def tile_picked_modres_mlpgelu_p_kernel(
         by_hand = ctx.enter_context(tc.tile_pool(name="by_hand", bufs=1))
         psum = ctx.enter_context(tc.psum_pool(name="psum", bufs=1))
 
-        def sbuf(name, shape, dtype, reuses=None):
-            return keep.tile(shape, dtype, name=name, tag=reuses or name, align_bytes=64)
+        def sbuf(name, shape, dtype):
+            return keep.tile(shape, dtype, name=name, align_bytes=64)
 
         def placed(name, shape, dtype, offset):
             return by_hand.tile(shape, dtype, name=name, offset=offset, align_bytes=64)
 
         x_scale_window = placed("x_scale_window", [P, T], U8, X_SCALES_AT)
         nc.gpsimd.memset(x_scale_window[:].bitcast(I32), 0)
-        w2_scale = sbuf("w2_scale", [P, N], U8)
-        nc.vector.memset(w2_scale[:].bitcast(I32), 0)
 
+        def load_x_scales(queue, q):
+            queue.dma_start(
+                x_scale_window[32 * q : 32 * q + 4 * PASSES, :].bitcast(I32),
+                x_scales[:, 4 * q : 4 * q + 4, :].bitcast(I32),
+            )
+
+        for q in range(2):
+            load_x_scales(nc.scalar, q)
         table_in = sbuf("table_in", [P, 16], F32)
         table_out = sbuf("table_out", [P, 16], F32)
-        nc.vector.memset(table_in[:], 0.0)
+        nc.gpsimd.memset(table_in[:], 0.0)
         nc.scalar.activation(table_out[:], table_in[:], GELU)
+
+        identity = sbuf("identity", [P, P], F32)
+        make_identity(nc, identity[:])
 
         offsets = sbuf("offsets", [P, S // 16], U16)
 
         def entries(lo, hi):
             return offsets[:, lo // 16 : hi // 16]
 
+        w1_rows = w1.rearrange("(g p j) c -> g p (j c)", g=PASSES, j=PACK)
         x_word_window = []
+        w1_raw = []
         for g in range(PASSES):
-            window = sbuf("x_word_window%d" % g, [P, T], U32)
-            nc.sync.dma_start(window[:].bitcast(I32), x_words[g].rearrange("p n j -> p (n j)").bitcast(I32))
-            x_word_window.append(window)
+            x_word_window.append(placed("x_word_window%d" % g, [P, T], U32, X_WORDS_AT + 4 * T * g))
+            nc.sync.dma_start(x_word_window[g][:].bitcast(I32), x_words[g].rearrange("p n j -> p (n j)").bitcast(I32))
             if g == 0:
                 nc.sync.dma_start(offsets[:], offs)
-        for q in range(QUADRANTS):
-            nc.scalar.dma_start(
-                x_scale_window[32 * q : 32 * q + 4 * PASSES, :].bitcast(I32),
-                x_scales[:, 4 * q : 4 * q + 4, :].bitcast(I32),
-            )
-        ones = sbuf("ones", [P, P], F32)
-        nc.vector.memset(ones[:], 1.0)
-        identity = sbuf("identity", [P, P], F32)
-        nc.gpsimd.affine_select(
-            out=identity[:], in_=ones[:], compare_op=IS_EQUAL, fill=0.0, base=0, pattern=[[-1, P]], channel_multiplier=1
-        )
-
-        w1_rows = w1.rearrange("(g p j) c -> g p j c", g=PASSES, j=PACK)
-        w1_raw = []
-        at = 0
-        for i, (g, lo, hi, on_vector) in enumerate(W1_PIECES):
-            piece = placed("w1_raw%d" % i, [P, PACK, hi - lo], F32, at)
-            at = at + 4 * PACK * (hi - lo)
-            nc.sync.dma_start(piece[:], w1_rows[g][:, :, lo:hi])
-            w1_raw.append(piece)
+                for q in range(2, QUADRANTS):
+                    load_x_scales(nc.sync, q)
+            w1_raw.append(placed("w1_raw%d" % g, [P, PACK * H], F32, W1_AT + 4 * PACK * H * g))
+            nc.sync.dma_start(w1_raw[g][:], w1_rows[g])
 
         x_word = [sbuf("x_word%d" % g, [P, S], U32) for g in range(PASSES)]
-        for g in range(PASSES):
-            nc.vector.tensor_copy(x_word[g][:], x_word_window[g][:].indirect(offsets[:]))
         x_scale = sbuf("x_scale", [P, S], U8)
         nc.vector.tensor_copy(x_scale[:], x_scale_window[:].indirect(offsets[:]))
+        for g in range(PASSES):
+            nc.vector.tensor_copy(x_word[g][:], x_word_window[g][:].indirect(offsets[:]))
 
-        rows = [sbuf("rows%d" % b, [P, T], F32) for b in range(BLOCKS)]
-        for b in range(BLOCKS):
-            nc.sync.dma_start(rows[b][:], res[P * b : P * (b + 1), :])
-        w2_word = sbuf("w2_word", [P, 2 * N], U8)
+        rows = [placed("rows0", [P, T], F32, X_WORDS_AT)]
+        nc.sync.dma_start(rows[0][:], res[0:P, :])
+
+        acc = [psum.tile([P, PACK, CHUNK], F32, name="acc%d" % c) for c in range(CHUNKS)]
+        w1_word = {}
+        w1_scale = {}
+
+        def quantise_w1(g):
+            src = w1_raw[g][:].rearrange("p (j m t) -> p m j t", j=PACK, t=PACK)
+            rounded = [
+                placed("w1_bf16_%d_%d" % (g, u), [P, 2, P, PACK], BF16, ROUNDED_AT + 2048 * (2 * g + u)) for u in range(2)
+            ]
+            dst = [rounded[u][:].rearrange("p t m j -> p m j t") for u in range(2)]
+            extra = EXTRA_ON_VECTOR[g]
+            nc.vector.tensor_copy(dst[0], src[:, :, :, 0:2])
+            if extra > 0:
+                nc.vector.tensor_copy(dst[1][:, 0:extra], src[:, 0:extra, :, 2:4])
+            nc.scalar.copy(dst[1][:, extra:P], src[:, extra:P, :, 2:4])
+            for u in range(2):
+                w1_word[g, u] = sbuf("w1_word%d_%d" % (g, u), [P, 2 * P], U32)
+                if g == 0:
+                    w1_scale[g, u] = placed("w1_scale%d_%d" % (g, u), [P, 2 * P], U8, X_SCALES_AT + 2 * P * u)
+                else:
+                    w1_scale[g, u] = sbuf("w1_scale%d_%d" % (g, u), [P, 2 * P], U8)
+                nc.vector.quantize_mx(
+                    out=w1_word[g, u][:].bitcast(FP8X4),
+                    scales=w1_scale[g, u][:],
+                    in_=rounded[u][:].rearrange("p t m j -> p (t m j)"),
+                )
+
+        def first_product(g, c):
+            cols = slice(CHUNK * c, CHUNK * (c + 1))
+            for t in range(PACK):
+                units = slice(P * (t % 2), P * (t % 2 + 1))
+                nc.tensor.matmul_mx(
+                    out=acc[c][:, t, :],
+                    lhsT=w1_word[g, t // 2][:, units].bitcast(FP8X4),
+                    lhsT_scale=w1_scale[g, t // 2][:, units],
+                    rhs=x_word[g][:, cols].bitcast(FP8X4),
+                    rhs_scale=x_scale[4 * g : P, cols],
+                    start=(g == 0 and t == 0),
+                    stop=(g == PASSES - 1 and t == PACK - 1),
+                )
+
+        quantise_w1(0)
+        for c in range(CHUNKS):
+            first_product(0, c)
+
+        rows.append(placed("rows1", [P, T], F32, W1_AT))
+        nc.sync.dma_start(rows[1][:], res[P : 2 * P, :])
+        w2_word = placed("w2_word", [P, 2 * N], U8, W1_AT + 4 * T)
         nc.sync.dma_start(w2_word[:].bitcast(I32), w2_words[0].bitcast(I32))
-        gate_first = sbuf("gate_first", [P, CHUNK], F32)
-        nc.sync.dma_start(gate_first[:], gate[:, 0:CHUNK])
+        w2_scale = placed("w2_scale", [P, N], U8, W1_AT + 4 * T + 2 * N)
+        nc.gpsimd.memset(w2_scale[:].bitcast(I32), 0)
         for q in range(QUADRANTS):
             nc.sync.dma_start(
                 w2_scale[32 * q : 32 * q + 4, :].bitcast(I32),
                 w2_scales[0][4 * q : 4 * q + 4, :].bitcast(I32),
             )
-        gate_by_partition = sbuf("gate_by_partition", [P, S // CHUNK - 1], F32)
+        gate_first = placed("gate_first", [P, CHUNK], F32, W1_AT + 4 * T + 4 * N)
+        nc.sync.dma_start(gate_first[:], gate[:, 0:CHUNK])
+        gate_by_partition = placed("gate_by_partition", [P, CHUNKS - 1], F32, W1_AT + 4 * T + 6 * N)
         with nc.allow_non_contiguous_dma(reason="one gate value a partition"):
             nc.sync.dma_start(gate_by_partition[:], gate[0, CHUNK:S].rearrange("(c p) -> p c", p=P))
 
-        w1_word = [sbuf("w1_word%d" % g, [P, H], U32) for g in range(PASSES)]
-        w1_scale = [sbuf("w1_scale%d" % g, [P, H], U8) for g in range(PASSES)]
-        for i, (g, lo, hi, on_vector) in enumerate(W1_PIECES):
-            width = (hi - lo) // PACK
-            rounded = sbuf("w1_bf16_%d" % i, [P, PACK, width, PACK], BF16)
-            src = w1_raw[i][:].rearrange("p j (m t) -> p m j t", t=PACK)
-            dst = rounded[:].rearrange("p t m j -> p m j t")
-            if on_vector > 0:
-                nc.vector.tensor_copy(dst[:, :, :, 0:on_vector], src[:, :, :, 0:on_vector])
-            if on_vector < PACK:
-                nc.scalar.copy(dst[:, :, :, on_vector:PACK], src[:, :, :, on_vector:PACK])
-            tiles_a_call = 2 if width == P else 1
-            for t in range(0, PACK, tiles_a_call):
-                cols = slice(P * t + lo // PACK, P * (t + tiles_a_call - 1) + hi // PACK)
-                nc.vector.quantize_mx(
-                    out=w1_word[g][:, cols].bitcast(FP8X4),
-                    scales=w1_scale[g][:, cols],
-                    in_=rounded[:, t : t + tiles_a_call].rearrange("p t m j -> p (t m j)"),
-                )
+        quantise_w1(1)
+        for c in range(CHUNKS):
+            first_product(1, c)
 
-        h_word = {}
-        h_scale = [sbuf("h_scale%d" % c, [P, CHUNK], U8) for c in range(S // CHUNK)]
+        old = [placed("old%d" % b, [P, S], F32, ROUNDED_AT + 2048 * (3 - b)) for b in range(BLOCKS)]
+        for b in range(BLOCKS):
+            nc.vector.tensor_copy(old[b][:], rows[b][:].indirect(offsets[:]))
 
-        def first_layer(c):
-            cols = slice(CHUNK * c, CHUNK * (c + 1))
-            acc = psum.tile([P, PACK, CHUNK], F32, name="acc%d" % c)
-            for t in range(PACK):
-                units = slice(P * t, P * (t + 1))
-                for g in range(PASSES):
-                    nc.tensor.matmul_mx(
-                        out=acc[:, t, :],
-                        lhsT=w1_word[g][:, units].bitcast(FP8X4),
-                        lhsT_scale=w1_scale[g][:, units],
-                        rhs=x_word[g][:, cols].bitcast(FP8X4),
-                        rhs_scale=x_scale[4 * g : P, cols],
-                        start=(g == 0),
-                        stop=(g == PASSES - 1),
-                    )
-            if c == 1:
-                h = placed("h%d" % c, [P, CHUNK, PACK], BF16, SHARED_AT)
+        h = []
+        for c in range(CHUNKS):
+            if c == HOLD_CHUNK:
+                h.append(placed("h%d" % c, [P, CHUNK, PACK], BF16, 0))
             else:
-                h = sbuf("h%d" % c, [P, CHUNK, PACK], BF16)
-            if c == 9:
-                h_word[c] = placed("h_word%d" % c, [P, CHUNK], U32, SHARED_AT)
-            else:
-                h_word[c] = sbuf("h_word%d" % c, [P, CHUNK], U32)
-            nc.scalar.activation(h[:], acc[:].rearrange("p t n -> p n t"), GELU)
+                h.append(sbuf("h%d" % c, [P, CHUNK, PACK], BF16))
+            nc.scalar.activation(h[c][:], acc[c][:].rearrange("p t n -> p n t"), GELU)
+        h_word = [sbuf("h_word%d" % c, [P, CHUNK], U32) for c in range(CHUNKS)]
+        h_scale = [sbuf("h_scale%d" % c, [P, CHUNK], U8) for c in range(CHUNKS)]
+        for c in range(CHUNKS):
             nc.vector.quantize_mx(
-                out=h_word[c][:].bitcast(FP8X4), scales=h_scale[c][:], in_=h[:].rearrange("p n t -> p (n t)")
+                out=h_word[c][:].bitcast(FP8X4), scales=h_scale[c][:], in_=h[c][:].rearrange("p n t -> p (n t)")
             )
 
-        def second_layer_first_chunk():
-            y = psum.tile([P, BLOCKS, CHUNK], F32, name="y0", tag="y", bufs=2)
-            for b in range(BLOCKS):
-                nc.tensor.matmul_mx(
-                    out=y[:, b, :],
-                    lhsT=w2_word[:, 2 * P * b : 2 * P * (b + 1)].bitcast(FP4X4),
-                    lhsT_scale=w2_scale[:, P * b : P * (b + 1)],
-                    rhs=h_word[0][:].bitcast(FP8X4),
-                    rhs_scale=h_scale[0][:],
-                    start=True,
-                    stop=True,
-                )
-            gated = [placed("gated_first%d" % b, [P, CHUNK], F32, SHARED_AT + 4 * CHUNK * b) for b in range(BLOCKS)]
-            for b in range(BLOCKS):
-                nc.vector.tensor_tensor(gated[b][:], y[:, b, :], gate_first[:], MULT)
-            return gated
+        y = psum.tile([P, BLOCKS, CHUNK], F32, name="y0")
+        for b in range(BLOCKS):
+            nc.tensor.matmul_mx(
+                out=y[:, b, :],
+                lhsT=w2_word[:, 2 * P * b : 2 * P * (b + 1)].bitcast(FP4X4),
+                lhsT_scale=w2_scale[:, P * b : P * (b + 1)],
+                rhs=h_word[0][:].bitcast(FP8X4),
+                rhs_scale=h_scale[0][:],
+                start=True,
+                stop=True,
+            )
+        gated_first = [placed("gated_first%d" % b, [P, CHUNK], F32, 4 * CHUNK * b) for b in range(BLOCKS)]
+        for b in range(BLOCKS):
+            nc.vector.tensor_tensor(gated_first[b][:], y[:, b, :], gate_first[:], MULT)
 
         gated_rest = sbuf("gated_rest", [P, BLOCKS, S - CHUNK], F32)
-
-        def second_layer_turned(c):
-            y_turned = psum.tile([P, N], F32, name="y%d" % c, tag="y", bufs=2)
+        gated_turned = {}
+        for c in range(1, CHUNKS):
+            y_turned = psum.tile([P, N], F32, name="y%d" % c, tag="bank%d" % c)
             nc.tensor.matmul_mx(
                 out=y_turned[:],
                 lhsT=h_word[c][:].bitcast(FP8X4),
@@ -195,49 +209,21 @@ def tile_picked_modres_mlpgelu_p_kernel(
                 start=True,
                 stop=True,
             )
-            gated_turned = sbuf("gated_turned%d" % c, [P, N], F32)
-            nc.scalar.activation(gated_turned[:], y_turned[:], COPY, scale=gate_by_partition[:, c - 1 : c])
-            back = psum.tile([P, BLOCKS, CHUNK], F32, name="back%d" % c, tag="back", bufs=2)
+            gated_turned[c] = sbuf("gated_turned%d" % c, [P, N], F32)
+            nc.scalar.activation(gated_turned[c][:], y_turned[:], COPY, scale=gate_by_partition[:, c - 1 : c])
+        for c in range(1, CHUNKS):
+            back = psum.tile([P, BLOCKS, CHUNK], F32, name="back%d" % c, tag="bank%d" % (c % (CHUNKS - 1) + 1))
             for b in range(BLOCKS):
-                nc.tensor.transpose(back[:, b, :], gated_turned[:, P * b : P * (b + 1)], identity[:])
+                nc.tensor.transpose(back[:, b, :], gated_turned[c][:, P * b : P * (b + 1)], identity[:])
             nc.scalar.copy(gated_rest[:, :, CHUNK * (c - 1) : CHUNK * c], back[:])
 
-        def look_up_res(name, b, lo, hi, reuses=None):
-            old = sbuf(name, [P, hi - lo], F32, reuses)
-            nc.vector.tensor_copy(old[:], rows[b][:].indirect(entries(lo, hi)))
-            return old
+        def put_back(b, lo, hi, gated):
+            nc.vector.tensor_tensor(rows[b][:].indirect(entries(lo, hi)), gated, old[b][:, lo:hi], ADD)
 
-        def put_back(b, lo, hi, gated, old):
-            nc.vector.tensor_tensor(rows[b][:].indirect(entries(lo, hi)), gated, old, ADD)
-
-        for i, width in enumerate((512, 512, 256)):
-            warm_up = psum.tile([P, width], F32, name="warm_up%d" % i, tag="back", bufs=2)
-            nc.tensor.matmul_mx(
-                out=warm_up[:],
-                lhsT=x_word[0][:, 0:P].bitcast(FP8X4),
-                lhsT_scale=x_scale[:, 0:P],
-                rhs=x_word[0][:, 0:width].bitcast(FP8X4),
-                rhs_scale=x_scale[:, 0:width],
-                start=True,
-                stop=True,
-            )
-
-        old0 = look_up_res("old0", 0, 0, S)
-        old1 = look_up_res("old1", 1, 0, S)
-        old = (old0, old1)
-        first_layer(0)
-        first_layer(1)
-        gated_first = second_layer_first_chunk()
-        first_layer(2)
-        second_layer_turned(1)
         for b in range(BLOCKS):
-            put_back(b, 0, CHUNK, gated_first[b][:], old[b][:, 0:CHUNK])
-        first_layer(3)
-        second_layer_turned(2)
-        second_layer_turned(3)
-
+            put_back(b, 0, CHUNK, gated_first[b][:])
         for lo, hi in ((CHUNK, HALF), (HALF, S)):
             for b in range(BLOCKS):
-                put_back(b, lo, hi, gated_rest[:, b, lo - CHUNK : hi - CHUNK], old[b][:, lo:hi])
+                put_back(b, lo, hi, gated_rest[:, b, lo - CHUNK : hi - CHUNK])
                 if hi == S:
                     nc.sync.dma_start(out[P * b : P * (b + 1), :], rows[b][:])

@@ -28,12 +28,11 @@ COPY = mybir.ActivationFunctionType.Copy
 ADD = mybir.AluOpType.add
 MULT = mybir.AluOpType.mult
 
-EXTRA_ON_VECTOR = (0, 32)
-HOLD_CHUNK = 3
+W1_PIECES = ((0, 0, H, (128, 0)), (1, 0, H // 2, (0, 0)), (1, H // 2, H, (64, 32)))
+H_GROUPS = ((0,), (1, 2), (3,))
 X_WORDS_AT = 1024
 X_SCALES_AT = X_WORDS_AT + 8 * T
 W1_AT = X_SCALES_AT + T
-ROUNDED_AT = W1_AT + 4 * PASSES * PACK * H
 
 
 def tile_picked_modres_mlpgelu_p_kernel(
@@ -75,9 +74,9 @@ def tile_picked_modres_mlpgelu_p_kernel(
         def entries(lo, hi):
             return offsets[:, lo // 16 : hi // 16]
 
-        w1_rows = w1.rearrange("(g p j) c -> g p (j c)", g=PASSES, j=PACK)
+        w1_rows = w1.rearrange("(g p j) c -> g p j c", g=PASSES, j=PACK)
         x_word_window = []
-        w1_raw = []
+        w1_raw = {}
         for g in range(PASSES):
             x_word_window.append(placed("x_word_window%d" % g, [P, T], U32, X_WORDS_AT + 4 * T * g))
             nc.sync.dma_start(x_word_window[g][:].bitcast(I32), x_words[g].rearrange("p n j -> p (n j)").bitcast(I32))
@@ -85,8 +84,10 @@ def tile_picked_modres_mlpgelu_p_kernel(
                 nc.sync.dma_start(offsets[:], offs)
                 for q in range(2, QUADRANTS):
                     load_x_scales(nc.sync, q)
-            w1_raw.append(placed("w1_raw%d" % g, [P, PACK * H], F32, W1_AT + 4 * PACK * H * g))
-            nc.sync.dma_start(w1_raw[g][:], w1_rows[g])
+            for i, (piece_pass, lo, hi, on_vector) in enumerate(W1_PIECES):
+                if piece_pass == g:
+                    w1_raw[i] = placed("w1_raw%d" % i, [P, PACK, hi - lo], F32, W1_AT + 4 * PACK * (H * g + lo))
+                    nc.sync.dma_start(w1_raw[i][:], w1_rows[g][:, :, lo:hi])
 
         x_word = [sbuf("x_word%d" % g, [P, S], U32) for g in range(PASSES)]
         x_scale = sbuf("x_scale", [P, S], U8)
@@ -100,33 +101,40 @@ def tile_picked_modres_mlpgelu_p_kernel(
         acc = [psum.tile([P, PACK, CHUNK], F32, name="acc%d" % c) for c in range(CHUNKS)]
         w1_word = {}
         w1_scale = {}
-
-        def quantise_w1(g):
-            src = w1_raw[g][:].rearrange("p (j m t) -> p m j t", j=PACK, t=PACK)
-            rounded = [
-                placed("w1_bf16_%d_%d" % (g, u), [P, 2, P, PACK], BF16, ROUNDED_AT + 2048 * (2 * g + u)) for u in range(2)
-            ]
-            dst = [rounded[u][:].rearrange("p t m j -> p m j t") for u in range(2)]
-            extra = EXTRA_ON_VECTOR[g]
-            nc.vector.tensor_copy(dst[0], src[:, :, :, 0:2])
-            if extra > 0:
-                nc.vector.tensor_copy(dst[1][:, 0:extra], src[:, 0:extra, :, 2:4])
-            nc.scalar.copy(dst[1][:, extra:P], src[:, extra:P, :, 2:4])
+        for g in range(PASSES):
             for u in range(2):
                 w1_word[g, u] = sbuf("w1_word%d_%d" % (g, u), [P, 2 * P], U32)
                 if g == 0:
                     w1_scale[g, u] = placed("w1_scale%d_%d" % (g, u), [P, 2 * P], U8, X_SCALES_AT + 2 * P * u)
                 else:
                     w1_scale[g, u] = sbuf("w1_scale%d_%d" % (g, u), [P, 2 * P], U8)
-                nc.vector.quantize_mx(
-                    out=w1_word[g, u][:].bitcast(FP8X4),
-                    scales=w1_scale[g, u][:],
-                    in_=rounded[u][:].rearrange("p t m j -> p (t m j)"),
-                )
+
+        def quantise_w1(i):
+            g, lo, hi, on_vector = W1_PIECES[i]
+            width = (hi - lo) // PACK
+            src = w1_raw[i][:].rearrange("p j (m t) -> p m j t", t=PACK)
+            rounded = [sbuf("w1_bf16_%d_%d" % (i, u), [P, 2, width, PACK], BF16) for u in range(2)]
+            dst = [rounded[u][:].rearrange("p t m j -> p m j t") for u in range(2)]
+            for u in range(2):
+                pair = src[:, :, :, 2 * u : 2 * u + 2]
+                if on_vector[u] > 0:
+                    nc.vector.tensor_copy(dst[u][:, 0 : on_vector[u]], pair[:, 0 : on_vector[u]])
+                if on_vector[u] < width:
+                    nc.scalar.copy(dst[u][:, on_vector[u] : width], pair[:, on_vector[u] : width])
+            tiles_a_call = 2 if width == P else 1
+            for u in range(2):
+                for t in range(0, 2, tiles_a_call):
+                    cols = slice(P * t + lo // PACK, P * (t + tiles_a_call - 1) + hi // PACK)
+                    nc.vector.quantize_mx(
+                        out=w1_word[g, u][:, cols].bitcast(FP8X4),
+                        scales=w1_scale[g, u][:, cols],
+                        in_=rounded[u][:, t : t + tiles_a_call].rearrange("p t m j -> p (t m j)"),
+                    )
 
         def first_product(g, c):
             cols = slice(CHUNK * c, CHUNK * (c + 1))
-            for t in range(PACK):
+            order = range(PACK) if g == 0 or c == 0 else range(PACK - 1, -1, -1)
+            for t in order:
                 units = slice(P * (t % 2), P * (t % 2 + 1))
                 nc.tensor.matmul_mx(
                     out=acc[c][:, t, :],
@@ -134,8 +142,8 @@ def tile_picked_modres_mlpgelu_p_kernel(
                     lhsT_scale=w1_scale[g, t // 2][:, units],
                     rhs=x_word[g][:, cols].bitcast(FP8X4),
                     rhs_scale=x_scale[4 * g : P, cols],
-                    start=(g == 0 and t == 0),
-                    stop=(g == PASSES - 1 and t == PACK - 1),
+                    start=(g == 0 and t == order[0]),
+                    stop=(g == PASSES - 1 and t == order[-1]),
                 )
 
         quantise_w1(0)
@@ -160,26 +168,30 @@ def tile_picked_modres_mlpgelu_p_kernel(
             nc.sync.dma_start(gate_by_partition[:], gate[0, CHUNK:S].rearrange("(c p) -> p c", p=P))
 
         quantise_w1(1)
+        quantise_w1(2)
         for c in range(CHUNKS):
             first_product(1, c)
 
-        old = [placed("old%d" % b, [P, S], F32, ROUNDED_AT + 2048 * (3 - b)) for b in range(BLOCKS)]
+        old = [sbuf("old%d" % b, [P, S], F32) for b in range(BLOCKS)]
         for b in range(BLOCKS):
             nc.vector.tensor_copy(old[b][:], rows[b][:].indirect(offsets[:]))
 
-        h = []
-        for c in range(CHUNKS):
-            if c == HOLD_CHUNK:
-                h.append(placed("h%d" % c, [P, CHUNK, PACK], BF16, 0))
-            else:
-                h.append(sbuf("h%d" % c, [P, CHUNK, PACK], BF16))
-            nc.scalar.activation(h[c][:], acc[c][:].rearrange("p t n -> p n t"), GELU)
-        h_word = [sbuf("h_word%d" % c, [P, CHUNK], U32) for c in range(CHUNKS)]
-        h_scale = [sbuf("h_scale%d" % c, [P, CHUNK], U8) for c in range(CHUNKS)]
-        for c in range(CHUNKS):
+        h_word = {}
+        h_scale = {}
+        for group in H_GROUPS:
+            h = sbuf("h%d" % group[0], [P, len(group), CHUNK, PACK], BF16)
+            for i, c in enumerate(group):
+                nc.scalar.activation(h[:, i], acc[c][:].rearrange("p t n -> p n t"), GELU)
+            words = sbuf("h_word%d" % group[0], [P, len(group), CHUNK], U32)
+            scales = sbuf("h_scale%d" % group[0], [P, len(group), CHUNK], U8)
             nc.vector.quantize_mx(
-                out=h_word[c][:].bitcast(FP8X4), scales=h_scale[c][:], in_=h[c][:].rearrange("p n t -> p (n t)")
+                out=words[:].rearrange("p c n -> p (c n)").bitcast(FP8X4),
+                scales=scales[:].rearrange("p c n -> p (c n)"),
+                in_=h[:].rearrange("p c n t -> p (c n t)"),
             )
+            for i, c in enumerate(group):
+                h_word[c] = words[:, i]
+                h_scale[c] = scales[:, i]
 
         y = psum.tile([P, BLOCKS, CHUNK], F32, name="y0")
         for b in range(BLOCKS):
@@ -187,12 +199,12 @@ def tile_picked_modres_mlpgelu_p_kernel(
                 out=y[:, b, :],
                 lhsT=w2_word[:, 2 * P * b : 2 * P * (b + 1)].bitcast(FP4X4),
                 lhsT_scale=w2_scale[:, P * b : P * (b + 1)],
-                rhs=h_word[0][:].bitcast(FP8X4),
-                rhs_scale=h_scale[0][:],
+                rhs=h_word[0].bitcast(FP8X4),
+                rhs_scale=h_scale[0],
                 start=True,
                 stop=True,
             )
-        gated_first = [placed("gated_first%d" % b, [P, CHUNK], F32, 4 * CHUNK * b) for b in range(BLOCKS)]
+        gated_first = [sbuf("gated_first%d" % b, [P, CHUNK], F32) for b in range(BLOCKS)]
         for b in range(BLOCKS):
             nc.vector.tensor_tensor(gated_first[b][:], y[:, b, :], gate_first[:], MULT)
 
@@ -202,8 +214,8 @@ def tile_picked_modres_mlpgelu_p_kernel(
             y_turned = psum.tile([P, N], F32, name="y%d" % c, tag="bank%d" % c)
             nc.tensor.matmul_mx(
                 out=y_turned[:],
-                lhsT=h_word[c][:].bitcast(FP8X4),
-                lhsT_scale=h_scale[c][:],
+                lhsT=h_word[c].bitcast(FP8X4),
+                lhsT_scale=h_scale[c],
                 rhs=w2_word[:].bitcast(FP4X4),
                 rhs_scale=w2_scale[:],
                 start=True,

@@ -28,7 +28,7 @@ COPY = mybir.ActivationFunctionType.Copy
 ADD = mybir.AluOpType.add
 MULT = mybir.AluOpType.mult
 
-W1_PIECES = ((0, 0, H, (128, 0)), (1, 0, H // 2, (0, 0)), (1, H // 2, H, (64, 32)))
+W1_PIECES = ((0, 0, H, (128, 0)), (1, 0, H, (128, 32)))
 H_GROUPS = ((0,), (1, 2), (3,))
 X_WORDS_AT = 1024
 X_SCALES_AT = X_WORDS_AT + 8 * T
@@ -168,7 +168,6 @@ def tile_picked_modres_mlpgelu_p_kernel(
             nc.sync.dma_start(gate_by_partition[:], gate[0, CHUNK:S].rearrange("(c p) -> p c", p=P))
 
         quantise_w1(1)
-        quantise_w1(2)
         for c in range(CHUNKS):
             first_product(1, c)
 

@@ -155,7 +155,7 @@ def tile_picked_modres_mlpgelu_p_kernel(
         w2_word = placed("w2_word", [P, 2 * N], U8, W1_AT + 4 * T)
         nc.sync.dma_start(w2_word[:].bitcast(I32), w2_words[0].bitcast(I32))
         w2_scale = placed("w2_scale", [P, N], U8, W1_AT + 4 * T + 2 * N)
-        nc.gpsimd.memset(w2_scale[:].bitcast(I32), 0)
+        nc.vector.memset(w2_scale[:].bitcast(I32), 0)
         for q in range(QUADRANTS):
             nc.sync.dma_start(
                 w2_scale[32 * q : 32 * q + 4, :].bitcast(I32),
@@ -203,9 +203,10 @@ def tile_picked_modres_mlpgelu_p_kernel(
                 start=True,
                 stop=True,
             )
-        gated_first = [sbuf("gated_first%d" % b, [P, CHUNK], F32) for b in range(BLOCKS)]
-        for b in range(BLOCKS):
-            nc.vector.tensor_tensor(gated_first[b][:], y[:, b, :], gate_first[:], MULT)
+        gated_first = sbuf("gated_first", [P, BLOCKS, CHUNK], F32)
+        nc.vector.tensor_tensor(
+            gated_first[:], y[:], gate_first[:].unsqueeze(1).to_broadcast([P, BLOCKS, CHUNK]), MULT
+        )
 
         gated_rest = sbuf("gated_rest", [P, BLOCKS, S - CHUNK], F32)
         gated_turned = {}
@@ -231,10 +232,9 @@ def tile_picked_modres_mlpgelu_p_kernel(
         def put_back(b, lo, hi, gated):
             nc.vector.tensor_tensor(rows[b][:].indirect(entries(lo, hi)), gated, old[b][:, lo:hi], ADD)
 
-        for b in range(BLOCKS):
-            put_back(b, 0, CHUNK, gated_first[b][:])
-        for lo, hi in ((CHUNK, HALF), (HALF, S)):
-            for b in range(BLOCKS):
-                put_back(b, lo, hi, gated_rest[:, b, lo - CHUNK : hi - CHUNK])
-                if hi == S:
-                    nc.sync.dma_start(out[P * b : P * (b + 1), :], rows[b][:])
+        for b in (1, 0):
+            put_back(b, 0, CHUNK, gated_first[:, b, :])
+        for b, lo, hi in ((1, CHUNK, HALF), (0, CHUNK, S), (1, HALF, S)):
+            put_back(b, lo, hi, gated_rest[:, b, lo - CHUNK : hi - CHUNK])
+            if hi == S:
+                nc.sync.dma_start(out[P * b : P * (b + 1), :], rows[b][:])

@@ -13,7 +13,6 @@ QUADRANTS = 4
 BLOCKS = N // P
 CHUNK = 128
 CHUNKS = S // CHUNK
-HALF = S // 2
 
 F32 = mybir.dt.float32
 BF16 = mybir.dt.bfloat16
@@ -33,6 +32,8 @@ H_GROUPS = ((0,), (1, 2), (3,))
 X_WORDS_AT = 1024
 X_SCALES_AT = X_WORDS_AT + 8 * T
 W1_AT = X_SCALES_AT + T
+CODES_AT = W1_AT + PASSES * 4 * PACK * H
+H_AT = CODES_AT + 4 * H
 
 
 def tile_picked_modres_mlpgelu_p_kernel(
@@ -98,12 +99,15 @@ def tile_picked_modres_mlpgelu_p_kernel(
         rows = [placed("rows0", [P, T], F32, X_WORDS_AT)]
         nc.sync.dma_start(rows[0][:], res[0:P, :])
 
-        acc = [psum.tile([P, PACK, CHUNK], F32, name="acc%d" % c) for c in range(CHUNKS)]
+        acc = [psum.tile([P, PACK, CHUNK], F32, name="acc%d" % c, tag="acc%d" % c) for c in range(CHUNKS)]
         w1_word = {}
         w1_scale = {}
         for g in range(PASSES):
             for u in range(2):
-                w1_word[g, u] = sbuf("w1_word%d_%d" % (g, u), [P, 2 * P], U32)
+                if g == 1:
+                    w1_word[g, u] = placed("w1_word1_%d" % u, [P, 2 * P], U32, CODES_AT + 8 * P * u)
+                else:
+                    w1_word[g, u] = sbuf("w1_word%d_%d" % (g, u), [P, 2 * P], U32)
                 if g == 0:
                     w1_scale[g, u] = placed("w1_scale%d_%d" % (g, u), [P, 2 * P], U8, X_SCALES_AT + 2 * P * u)
                 else:
@@ -171,17 +175,30 @@ def tile_picked_modres_mlpgelu_p_kernel(
         for c in range(CHUNKS):
             first_product(1, c)
 
-        old = [sbuf("old%d" % b, [P, S], F32) for b in range(BLOCKS)]
-        for b in range(BLOCKS):
-            nc.vector.tensor_copy(old[b][:], rows[b][:].indirect(offsets[:]))
+        old0 = sbuf("old0", [P, S], F32)
+        nc.vector.tensor_copy(old0[:], rows[0][:].indirect(offsets[:]))
+        old1_first = sbuf("old1_first", [P, CHUNK], F32)
+        nc.vector.tensor_copy(old1_first[:], rows[1][:].indirect(entries(0, CHUNK)))
+        old1_last = placed("old1_last", [P, S - CHUNK], F32, CODES_AT)
+
+        def old(b, lo, hi):
+            if b == 0:
+                return old0[:, lo:hi]
+            return old1_first[:, lo:hi] if lo < CHUNK else old1_last[:, lo - CHUNK : hi - CHUNK]
 
         h_word = {}
         h_scale = {}
         for group in H_GROUPS:
-            h = sbuf("h%d" % group[0], [P, len(group), CHUNK, PACK], BF16)
+            if group[0] == CHUNKS - 1:
+                h = placed("h3", [P, 1, CHUNK, PACK], BF16, H_AT)
+            else:
+                h = sbuf("h%d" % group[0], [P, len(group), CHUNK, PACK], BF16)
             for i, c in enumerate(group):
                 nc.scalar.activation(h[:, i], acc[c][:].rearrange("p t n -> p n t"), GELU)
-            words = sbuf("h_word%d" % group[0], [P, len(group), CHUNK], U32)
+            if group[0] == 0:
+                words = placed("h_word0", [P, 1, CHUNK], U32, H_AT)
+            else:
+                words = sbuf("h_word%d" % group[0], [P, len(group), CHUNK], U32)
             scales = sbuf("h_scale%d" % group[0], [P, len(group), CHUNK], U8)
             nc.vector.quantize_mx(
                 out=words[:].rearrange("p c n -> p (c n)").bitcast(FP8X4),
@@ -191,22 +208,24 @@ def tile_picked_modres_mlpgelu_p_kernel(
             for i, c in enumerate(group):
                 h_word[c] = words[:, i]
                 h_scale[c] = scales[:, i]
+            if group[0] == 0:
+                nc.vector.tensor_copy(old1_last[:], rows[1][:].indirect(entries(CHUNK, S)))
+                y = psum.tile([P, BLOCKS, CHUNK], F32, name="y0")
+                for b in range(BLOCKS):
+                    nc.tensor.matmul_mx(
+                        out=y[:, b, :],
+                        lhsT=w2_word[:, 2 * P * b : 2 * P * (b + 1)].bitcast(FP4X4),
+                        lhsT_scale=w2_scale[:, P * b : P * (b + 1)],
+                        rhs=h_word[0].bitcast(FP8X4),
+                        rhs_scale=h_scale[0],
+                        start=True,
+                        stop=True,
+                    )
+                gated_first = sbuf("gated_first", [P, BLOCKS, CHUNK], F32)
+                nc.vector.tensor_tensor(
+                    gated_first[:], y[:], gate_first[:].unsqueeze(1).to_broadcast([P, BLOCKS, CHUNK]), MULT
+                )
 
-        y = psum.tile([P, BLOCKS, CHUNK], F32, name="y0")
-        for b in range(BLOCKS):
-            nc.tensor.matmul_mx(
-                out=y[:, b, :],
-                lhsT=w2_word[:, 2 * P * b : 2 * P * (b + 1)].bitcast(FP4X4),
-                lhsT_scale=w2_scale[:, P * b : P * (b + 1)],
-                rhs=h_word[0].bitcast(FP8X4),
-                rhs_scale=h_scale[0],
-                start=True,
-                stop=True,
-            )
-        gated_first = sbuf("gated_first", [P, BLOCKS, CHUNK], F32)
-        nc.vector.tensor_tensor(
-            gated_first[:], y[:], gate_first[:].unsqueeze(1).to_broadcast([P, BLOCKS, CHUNK]), MULT
-        )
 
         gated_rest = sbuf("gated_rest", [P, BLOCKS, S - CHUNK], F32)
         gated_turned = {}
@@ -224,17 +243,17 @@ def tile_picked_modres_mlpgelu_p_kernel(
             gated_turned[c] = sbuf("gated_turned%d" % c, [P, N], F32)
             nc.scalar.activation(gated_turned[c][:], y_turned[:], COPY, scale=gate_by_partition[:, c - 1 : c])
         for c in range(1, CHUNKS):
-            back = psum.tile([P, BLOCKS, CHUNK], F32, name="back%d" % c, tag="bank%d" % (c % (CHUNKS - 1) + 1))
+            back = psum.tile([P, BLOCKS, CHUNK], F32, name="back%d" % c, tag="acc%d" % (c - 1))
             for b in range(BLOCKS):
                 nc.tensor.transpose(back[:, b, :], gated_turned[c][:, P * b : P * (b + 1)], identity[:])
             nc.scalar.copy(gated_rest[:, :, CHUNK * (c - 1) : CHUNK * c], back[:])
 
         def put_back(b, lo, hi, gated):
-            nc.vector.tensor_tensor(rows[b][:].indirect(entries(lo, hi)), gated, old[b][:, lo:hi], ADD)
+            nc.vector.tensor_tensor(rows[b][:].indirect(entries(lo, hi)), gated, old(b, lo, hi), ADD)
 
         for b in (1, 0):
             put_back(b, 0, CHUNK, gated_first[:, b, :])
-        for b, lo, hi in ((1, CHUNK, HALF), (0, CHUNK, S), (1, HALF, S)):
+        for b, lo, hi in ((1, CHUNK, 2 * CHUNK), (0, CHUNK, S), (1, 2 * CHUNK, S)):
             put_back(b, lo, hi, gated_rest[:, b, lo - CHUNK : hi - CHUNK])
             if hi == S:
                 nc.sync.dma_start(out[P * b : P * (b + 1), :], rows[b][:])

@@ -27,13 +27,7 @@ COPY = mybir.ActivationFunctionType.Copy
 ADD = mybir.AluOpType.add
 MULT = mybir.AluOpType.mult
 
-W1_PIECES = ((0, 0, H, (128, 0)), (1, 0, H, (128, 32)))
-H_GROUPS = ((0,), (1, 2), (3,))
-X_WORDS_AT = 1024
-X_SCALES_AT = X_WORDS_AT + 8 * T
-W1_AT = X_SCALES_AT + T
-CODES_AT = W1_AT + PASSES * 4 * PACK * H
-H_AT = CODES_AT + 4 * H
+EXTRA_ON_VECTOR = (0, 0)
 
 
 def tile_picked_modres_mlpgelu_p_kernel(
@@ -42,16 +36,20 @@ def tile_picked_modres_mlpgelu_p_kernel(
     nc = tc.nc
     with ExitStack() as ctx:
         keep = ctx.enter_context(tc.tile_pool(name="keep", bufs=1))
+        shared = ctx.enter_context(tc.tile_pool(name="shared", bufs=1))
         by_hand = ctx.enter_context(tc.tile_pool(name="by_hand", bufs=1))
         psum = ctx.enter_context(tc.psum_pool(name="psum", bufs=1))
 
         def sbuf(name, shape, dtype):
             return keep.tile(shape, dtype, name=name, align_bytes=64)
 
+        def reused(name, shape, dtype, tag):
+            return shared.tile(shape, dtype, name=name, tag=tag, align_bytes=64)
+
         def placed(name, shape, dtype, offset):
             return by_hand.tile(shape, dtype, name=name, offset=offset, align_bytes=64)
 
-        x_scale_window = placed("x_scale_window", [P, T], U8, X_SCALES_AT)
+        x_scale_window = reused("x_scale_window", [P, T], U8, "scale_window")
         nc.gpsimd.memset(x_scale_window[:].bitcast(I32), 0)
 
         def load_x_scales(queue, q):
@@ -66,6 +64,8 @@ def tile_picked_modres_mlpgelu_p_kernel(
         table_out = sbuf("table_out", [P, 16], F32)
         nc.gpsimd.memset(table_in[:], 0.0)
         nc.scalar.activation(table_out[:], table_in[:], GELU)
+        w2_scale = sbuf("w2_scale", [P, N], U8)
+        nc.gpsimd.memset(w2_scale[:].bitcast(I32), 0)
 
         identity = sbuf("identity", [P, P], F32)
         make_identity(nc, identity[:])
@@ -75,185 +75,158 @@ def tile_picked_modres_mlpgelu_p_kernel(
         def entries(lo, hi):
             return offsets[:, lo // 16 : hi // 16]
 
-        w1_rows = w1.rearrange("(g p j) c -> g p j c", g=PASSES, j=PACK)
-        x_word_window = []
-        w1_raw = {}
-        for g in range(PASSES):
-            x_word_window.append(placed("x_word_window%d" % g, [P, T], U32, X_WORDS_AT + 4 * T * g))
+        x_word_window = [sbuf("x_word_window%d" % g, [P, T], U32) for g in range(PASSES)]
+
+        def load_x_words(g):
             nc.sync.dma_start(x_word_window[g][:].bitcast(I32), x_words[g].rearrange("p n j -> p (n j)").bitcast(I32))
+
+        load_x_words(0)
+        nc.sync.dma_start(offsets[:], offs)
+        for q in range(2, QUADRANTS):
+            load_x_scales(nc.sync, q)
+        w1_rows = w1.rearrange("(g p j) c -> g p j c", g=PASSES, j=PACK)
+        w1_raw = [sbuf("w1_raw0", [P, PACK, H], F32), placed("w1_raw1", [P, PACK, H], F32, 12288)]
+        for g in range(PASSES):
+            nc.sync.dma_start(w1_raw[g][:], w1_rows[g])
             if g == 0:
-                nc.sync.dma_start(offsets[:], offs)
-                for q in range(2, QUADRANTS):
-                    load_x_scales(nc.sync, q)
-            for i, (piece_pass, lo, hi, on_vector) in enumerate(W1_PIECES):
-                if piece_pass == g:
-                    w1_raw[i] = placed("w1_raw%d" % i, [P, PACK, hi - lo], F32, W1_AT + 4 * PACK * (H * g + lo))
-                    nc.sync.dma_start(w1_raw[i][:], w1_rows[g][:, :, lo:hi])
+                gate_by_four = sbuf("gate_by_four", [P, CHUNKS], F32)
+                nc.sync.dma_start(gate_by_four[:], gate[0].rearrange("(p c) -> p c", p=P))
+        load_x_words(1)
 
-        x_word = [sbuf("x_word%d" % g, [P, S], U32) for g in range(PASSES)]
-        x_scale = sbuf("x_scale", [P, S], U8)
-        nc.vector.tensor_copy(x_scale[:], x_scale_window[:].indirect(offsets[:]))
-        for g in range(PASSES):
-            nc.vector.tensor_copy(x_word[g][:], x_word_window[g][:].indirect(offsets[:]))
-
-        rows = [placed("rows0", [P, T], F32, X_WORDS_AT)]
-        nc.sync.dma_start(rows[0][:], res[0:P, :])
-
-        acc = [psum.tile([P, PACK, CHUNK], F32, name="acc%d" % c, tag="acc%d" % c) for c in range(CHUNKS)]
-        w1_word = {}
-        w1_scale = {}
-        for g in range(PASSES):
-            for u in range(2):
-                if g == 1:
-                    w1_word[g, u] = placed("w1_word1_%d" % u, [P, 2 * P], U32, CODES_AT + 8 * P * u)
-                else:
-                    w1_word[g, u] = sbuf("w1_word%d_%d" % (g, u), [P, 2 * P], U32)
-                if g == 0:
-                    w1_scale[g, u] = placed("w1_scale%d_%d" % (g, u), [P, 2 * P], U8, X_SCALES_AT + 2 * P * u)
-                else:
-                    w1_scale[g, u] = sbuf("w1_scale%d_%d" % (g, u), [P, 2 * P], U8)
-
-        def quantise_w1(i):
-            g, lo, hi, on_vector = W1_PIECES[i]
-            width = (hi - lo) // PACK
-            src = w1_raw[i][:].rearrange("p j (m t) -> p m j t", t=PACK)
-            rounded = [sbuf("w1_bf16_%d_%d" % (i, u), [P, 2, width, PACK], BF16) for u in range(2)]
-            dst = [rounded[u][:].rearrange("p t m j -> p m j t") for u in range(2)]
-            for u in range(2):
-                pair = src[:, :, :, 2 * u : 2 * u + 2]
-                if on_vector[u] > 0:
-                    nc.vector.tensor_copy(dst[u][:, 0 : on_vector[u]], pair[:, 0 : on_vector[u]])
-                if on_vector[u] < width:
-                    nc.scalar.copy(dst[u][:, on_vector[u] : width], pair[:, on_vector[u] : width])
-            tiles_a_call = 2 if width == P else 1
-            for u in range(2):
-                for t in range(0, 2, tiles_a_call):
-                    cols = slice(P * t + lo // PACK, P * (t + tiles_a_call - 1) + hi // PACK)
-                    nc.vector.quantize_mx(
-                        out=w1_word[g, u][:, cols].bitcast(FP8X4),
-                        scales=w1_scale[g, u][:, cols],
-                        in_=rounded[u][:, t : t + tiles_a_call].rearrange("p t m j -> p (t m j)"),
-                    )
-
-        def first_product(g, c):
-            cols = slice(CHUNK * c, CHUNK * (c + 1))
-            order = range(PACK) if g == 0 or c == 0 else range(PACK - 1, -1, -1)
-            for t in order:
-                units = slice(P * (t % 2), P * (t % 2 + 1))
-                nc.tensor.matmul_mx(
-                    out=acc[c][:, t, :],
-                    lhsT=w1_word[g, t // 2][:, units].bitcast(FP8X4),
-                    lhsT_scale=w1_scale[g, t // 2][:, units],
-                    rhs=x_word[g][:, cols].bitcast(FP8X4),
-                    rhs_scale=x_scale[4 * g : P, cols],
-                    start=(g == 0 and t == order[0]),
-                    stop=(g == PASSES - 1 and t == order[-1]),
-                )
-
-        quantise_w1(0)
-        for c in range(CHUNKS):
-            first_product(0, c)
-
-        rows.append(placed("rows1", [P, T], F32, W1_AT))
-        nc.sync.dma_start(rows[1][:], res[P : 2 * P, :])
-        w2_word = placed("w2_word", [P, 2 * N], U8, W1_AT + 4 * T)
+        rows_s = sbuf("rows_s", [P, T], F32)
+        nc.sync.dma_start(rows_s[:], res[P : 2 * P, :])
+        rows_v = sbuf("rows_v", [P, T], F32)
+        nc.sync.dma_start(rows_v[:], res[0:P, :])
+        w2_word = sbuf("w2_word", [P, 2 * N], U8)
         nc.sync.dma_start(w2_word[:].bitcast(I32), w2_words[0].bitcast(I32))
-        w2_scale = placed("w2_scale", [P, N], U8, W1_AT + 4 * T + 2 * N)
-        nc.vector.memset(w2_scale[:].bitcast(I32), 0)
         for q in range(QUADRANTS):
             nc.sync.dma_start(
                 w2_scale[32 * q : 32 * q + 4, :].bitcast(I32),
                 w2_scales[0][4 * q : 4 * q + 4, :].bitcast(I32),
             )
-        gate_first = placed("gate_first", [P, CHUNK], F32, W1_AT + 4 * T + 4 * N)
-        nc.sync.dma_start(gate_first[:], gate[:, 0:CHUNK])
-        gate_by_partition = placed("gate_by_partition", [P, CHUNKS - 1], F32, W1_AT + 4 * T + 6 * N)
-        with nc.allow_non_contiguous_dma(reason="one gate value a partition"):
-            nc.sync.dma_start(gate_by_partition[:], gate[0, CHUNK:S].rearrange("(c p) -> p c", p=P))
 
-        quantise_w1(1)
-        for c in range(CHUNKS):
-            first_product(1, c)
+        x_scale = sbuf("x_scale", [P, S], U8)
+        nc.vector.tensor_copy(x_scale[:], x_scale_window[:].indirect(offsets[:]))
+        x_word0 = sbuf("x_word0", [P, S], U32)
+        nc.vector.tensor_copy(x_word0[:], x_word_window[0][:].indirect(offsets[:]))
 
-        old0 = sbuf("old0", [P, S], F32)
-        nc.vector.tensor_copy(old0[:], rows[0][:].indirect(offsets[:]))
-        old1_first = sbuf("old1_first", [P, CHUNK], F32)
-        nc.vector.tensor_copy(old1_first[:], rows[1][:].indirect(entries(0, CHUNK)))
-        old1_last = placed("old1_last", [P, S - CHUNK], F32, CODES_AT)
+        acc = [psum.tile([P, PACK, CHUNK], F32, name="acc%d" % c, tag="acc%d" % c) for c in range(CHUNKS)]
+        w1_word = {}
+        w1_scale = {}
 
-        def old(b, lo, hi):
-            if b == 0:
-                return old0[:, lo:hi]
-            return old1_first[:, lo:hi] if lo < CHUNK else old1_last[:, lo - CHUNK : hi - CHUNK]
+        x_word1 = {}
 
-        h_word = {}
-        h_scale = {}
-        for group in H_GROUPS:
-            if group[0] == CHUNKS - 1:
-                h = placed("h3", [P, 1, CHUNK, PACK], BF16, H_AT)
+        def gather_x1(c):
+            if c == 0:
+                x_word1[c] = sbuf("x_word1_0", [P, CHUNK], U32)
             else:
-                h = sbuf("h%d" % group[0], [P, len(group), CHUNK, PACK], BF16)
-            for i, c in enumerate(group):
-                nc.scalar.activation(h[:, i], acc[c][:].rearrange("p t n -> p n t"), GELU)
-            if group[0] == 0:
-                words = placed("h_word0", [P, 1, CHUNK], U32, H_AT)
+                x_word1[c] = placed("x_word1_%d" % c, [P, CHUNK], U32, 1024 + 512 * c)
+            nc.vector.tensor_copy(x_word1[c][:], x_word_window[1][:].indirect(entries(CHUNK * c, CHUNK * (c + 1))))
+
+        def quantise_w1(g):
+            src = w1_raw[g][:].rearrange("p j (m t) -> p m j t", t=PACK)
+            rounded = [sbuf("w1_bf16_%d_0" % g, [P, 2, P, PACK], BF16)]
+            if g == 0:
+                rounded.append(sbuf("w1_bf16_0_1", [P, 2, P, PACK], BF16))
             else:
-                words = sbuf("h_word%d" % group[0], [P, len(group), CHUNK], U32)
-            scales = sbuf("h_scale%d" % group[0], [P, len(group), CHUNK], U8)
-            nc.vector.quantize_mx(
-                out=words[:].rearrange("p c n -> p (c n)").bitcast(FP8X4),
-                scales=scales[:].rearrange("p c n -> p (c n)"),
-                in_=h[:].rearrange("p c n t -> p (c n t)"),
-            )
-            for i, c in enumerate(group):
-                h_word[c] = words[:, i]
-                h_scale[c] = scales[:, i]
-            if group[0] == 0:
-                nc.vector.tensor_copy(old1_last[:], rows[1][:].indirect(entries(CHUNK, S)))
-                y = psum.tile([P, BLOCKS, CHUNK], F32, name="y0")
-                for b in range(BLOCKS):
-                    nc.tensor.matmul_mx(
-                        out=y[:, b, :],
-                        lhsT=w2_word[:, 2 * P * b : 2 * P * (b + 1)].bitcast(FP4X4),
-                        lhsT_scale=w2_scale[:, P * b : P * (b + 1)],
-                        rhs=h_word[0].bitcast(FP8X4),
-                        rhs_scale=h_scale[0],
-                        start=True,
-                        stop=True,
-                    )
-                gated_first = sbuf("gated_first", [P, BLOCKS, CHUNK], F32)
-                nc.vector.tensor_tensor(
-                    gated_first[:], y[:], gate_first[:].unsqueeze(1).to_broadcast([P, BLOCKS, CHUNK]), MULT
+                rounded.append(placed("w1_bf16_1_1", [P, 2, P, PACK], BF16, 1024))
+            dst = [rounded[u][:].rearrange("p t m j -> p m j t") for u in range(2)]
+            nc.vector.tensor_copy(dst[0], src[:, :, :, 0:2])
+            extra = EXTRA_ON_VECTOR[g]
+            if extra > 0:
+                nc.vector.tensor_copy(dst[1][:, 0:extra], src[:, 0:extra, :, 2:4])
+            nc.scalar.copy(dst[1][:, extra:P], src[:, extra:P, :, 2:4])
+            for u in range(2):
+                if (g, u) == (1, 1):
+                    gather_x1(0)
+                w1_word[g, u] = sbuf("w1_word%d_%d" % (g, u), [P, 2 * P], U32)
+                if (g, u) == (0, 0):
+                    w1_scale[g, u] = reused("w1_scale0_0", [P, 2 * P], U8, "scale_window")
+                else:
+                    w1_scale[g, u] = sbuf("w1_scale%d_%d" % (g, u), [P, 2 * P], U8)
+                nc.vector.quantize_mx(
+                    out=w1_word[g, u][:].bitcast(FP8X4),
+                    scales=w1_scale[g, u][:],
+                    in_=rounded[u][:].rearrange("p t m j -> p (t m j)"),
                 )
 
+        def first_product(g, c, words):
+            for t in range(PACK):
+                units = slice(P * (t % 2), P * (t % 2 + 1))
+                nc.tensor.matmul_mx(
+                    out=acc[c][:, t, :],
+                    lhsT=w1_word[g, t // 2][:, units].bitcast(FP8X4),
+                    lhsT_scale=w1_scale[g, t // 2][:, units],
+                    rhs=words.bitcast(FP8X4),
+                    rhs_scale=x_scale[4 * g : P, CHUNK * c : CHUNK * (c + 1)],
+                    start=(g == 0 and t == 0),
+                    stop=(g == PASSES - 1 and t == PACK - 1),
+                )
 
-        gated_rest = sbuf("gated_rest", [P, BLOCKS, S - CHUNK], F32)
-        gated_turned = {}
+        spread = psum.tile([P, CHUNKS, P], F32, name="spread", tag="y3")
+        for c in range(CHUNKS):
+            nc.tensor.transpose(spread[:, c, :], gate_by_four[:, c : c + 1].to_broadcast([P, P]), identity[:])
+        quantise_w1(0)
+        for c in range(CHUNKS):
+            first_product(0, c, x_word0[:, CHUNK * c : CHUNK * (c + 1)])
+        quantise_w1(1)
+        gates = placed("gates", [P, S], F32, 12288)
+        nc.scalar.copy(gates[:].rearrange("p (n c) -> p n c", c=CHUNKS), spread[:].rearrange("p c n -> p n c"))
+        first_product(1, 0, x_word1[0][:])
         for c in range(1, CHUNKS):
-            y_turned = psum.tile([P, N], F32, name="y%d" % c, tag="bank%d" % c)
-            nc.tensor.matmul_mx(
-                out=y_turned[:],
-                lhsT=h_word[c].bitcast(FP8X4),
-                lhsT_scale=h_scale[c],
-                rhs=w2_word[:].bitcast(FP4X4),
-                rhs_scale=w2_scale[:],
-                start=True,
-                stop=True,
-            )
-            gated_turned[c] = sbuf("gated_turned%d" % c, [P, N], F32)
-            nc.scalar.activation(gated_turned[c][:], y_turned[:], COPY, scale=gate_by_partition[:, c - 1 : c])
-        for c in range(1, CHUNKS):
-            back = psum.tile([P, BLOCKS, CHUNK], F32, name="back%d" % c, tag="acc%d" % (c - 1))
+            gather_x1(c)
+            first_product(1, c, x_word1[c][:])
+        old_s = [placed("old_s0", [P, 2 * CHUNK], F32, 512)]
+        nc.vector.tensor_copy(old_s[0][:], rows_s[:].indirect(entries(0, 2 * CHUNK)))
+
+        gated = sbuf("gated", [P, BLOCKS * S], F32)
+        summed = [sbuf("summed0", [P, 2 * CHUNK], F32), sbuf("summed1", [P, 2 * CHUNK], F32)]
+        for c in range(CHUNKS):
+            cols = slice(CHUNK * c, CHUNK * (c + 1))
+            if c == 0:
+                h = placed("h0", [P, CHUNK, PACK], BF16, 5120)
+            elif c == 3:
+                h = placed("h3", [P, CHUNK, PACK], BF16, 7168)
+            else:
+                h = sbuf("h%d" % c, [P, CHUNK, PACK], BF16)
+            nc.scalar.activation(h[:], acc[c][:].rearrange("p t n -> p n t"), GELU)
+            if c == 0:
+                h_word = placed("h_word0", [P, CHUNK], U32, 7168)
+            elif c == 1:
+                h_word = placed("h_word1", [P, CHUNK], U32, 8192)
+            else:
+                h_word = sbuf("h_word%d" % c, [P, CHUNK], U32)
+            h_scale = sbuf("h_scale%d" % c, [P, CHUNK], U8)
+            nc.vector.quantize_mx(out=h_word[:].bitcast(FP8X4), scales=h_scale[:], in_=h[:].rearrange("p n t -> p (n t)"))
+            y = psum.tile([P, BLOCKS, CHUNK], F32, name="y%d" % c, tag="y%d" % c)
             for b in range(BLOCKS):
-                nc.tensor.transpose(back[:, b, :], gated_turned[c][:, P * b : P * (b + 1)], identity[:])
-            nc.scalar.copy(gated_rest[:, :, CHUNK * (c - 1) : CHUNK * c], back[:])
+                nc.tensor.matmul_mx(
+                    out=y[:, b, :],
+                    lhsT=w2_word[:, 2 * P * b : 2 * P * (b + 1)].bitcast(FP4X4),
+                    lhsT_scale=w2_scale[:, P * b : P * (b + 1)],
+                    rhs=h_word[:].bitcast(FP8X4),
+                    rhs_scale=h_scale[:],
+                    start=True,
+                    stop=True,
+                )
+            if c == 0:
+                old_s.append(placed("old_s1", [P, 2 * CHUNK], F32, 5120))
+                nc.vector.tensor_copy(old_s[1][:], rows_s[:].indirect(entries(2 * CHUNK, S)))
+            nc.vector.tensor_tensor(
+                gated[:].rearrange("p (b s) -> p b s", b=BLOCKS)[:, :, cols],
+                y[:],
+                gates[:, cols].unsqueeze(1).to_broadcast([P, BLOCKS, CHUNK]),
+                MULT,
+            )
+            if c % 2 == 1:
+                lo, hi = CHUNK * (c - 1), CHUNK * (c + 1)
+                nc.vector.tensor_tensor(summed[c // 2][:], gated[:, S + lo : S + hi], old_s[c // 2][:], ADD)
 
-        def put_back(b, lo, hi, gated):
-            nc.vector.tensor_tensor(rows[b][:].indirect(entries(lo, hi)), gated, old(b, lo, hi), ADD)
+        old_v = placed("old_v", [P, S], F32, 8192)
+        nc.scalar.activation(old_v[:], rows_v[:].indirect(offsets[:]), COPY)
+        for lo in range(0, S, 2 * CHUNK):
+            nc.scalar.activation(rows_s[:].indirect(entries(lo, lo + 2 * CHUNK)), summed[lo // (2 * CHUNK)][:], COPY)
+        nc.sync.dma_start(out[P : 2 * P, :], rows_s[:])
 
-        for b in (1, 0):
-            put_back(b, 0, CHUNK, gated_first[:, b, :])
-        for b, lo, hi in ((1, CHUNK, 2 * CHUNK), (0, CHUNK, S), (1, 2 * CHUNK, S)):
-            put_back(b, lo, hi, gated_rest[:, b, lo - CHUNK : hi - CHUNK])
-            if hi == S:
-                nc.sync.dma_start(out[P * b : P * (b + 1), :], rows[b][:])
+        nc.vector.tensor_tensor(rows_v[:].indirect(offsets[:]), gated[:, 0:S], old_v[:], ADD)
+        nc.sync.dma_start(out[0:P, :], rows_v[:])

@@ -1,7 +1,6 @@
 from contextlib import ExitStack
 
 import concourse.mybir as mybir
-from concourse.masks import make_identity
 
 K, T, S, H, N = 1024, 1024, 512, 512, 256
 FLOPS = 2 * S * (K * H + H * N)
@@ -28,6 +27,7 @@ ADD = mybir.AluOpType.add
 MULT = mybir.AluOpType.mult
 
 EXTRA_ON_VECTOR = (0, 0)
+OLD_ON_VECTOR = 192
 
 
 def tile_picked_modres_mlpgelu_p_kernel(
@@ -67,9 +67,6 @@ def tile_picked_modres_mlpgelu_p_kernel(
         w2_scale = sbuf("w2_scale", [P, N], U8)
         nc.gpsimd.memset(w2_scale[:].bitcast(I32), 0)
 
-        identity = sbuf("identity", [P, P], F32)
-        make_identity(nc, identity[:])
-
         offsets = sbuf("offsets", [P, S // 16], U16)
 
         def entries(lo, hi):
@@ -85,18 +82,17 @@ def tile_picked_modres_mlpgelu_p_kernel(
         for q in range(2, QUADRANTS):
             load_x_scales(nc.sync, q)
         w1_rows = w1.rearrange("(g p j) c -> g p j c", g=PASSES, j=PACK)
-        w1_raw = [sbuf("w1_raw0", [P, PACK, H], F32), placed("w1_raw1", [P, PACK, H], F32, 12288)]
+        w1_raw = [sbuf("w1_raw%d" % g, [P, PACK, H], F32) for g in range(PASSES)]
         for g in range(PASSES):
             nc.sync.dma_start(w1_raw[g][:], w1_rows[g])
-            if g == 0:
-                gate_by_four = sbuf("gate_by_four", [P, CHUNKS], F32)
-                nc.sync.dma_start(gate_by_four[:], gate[0].rearrange("(p c) -> p c", p=P))
         load_x_words(1)
 
         rows_s = sbuf("rows_s", [P, T], F32)
         nc.sync.dma_start(rows_s[:], res[P : 2 * P, :])
         rows_v = sbuf("rows_v", [P, T], F32)
         nc.sync.dma_start(rows_v[:], res[0:P, :])
+        gates = [sbuf("gates%d" % u, [P, S // 2], F32) for u in range(2)]
+        nc.sync.dma_start(gates[0][:], gate[:, 0 : S // 2])
         w2_word = sbuf("w2_word", [P, 2 * N], U8)
         nc.sync.dma_start(w2_word[:].bitcast(I32), w2_words[0].bitcast(I32))
         for q in range(QUADRANTS):
@@ -104,6 +100,8 @@ def tile_picked_modres_mlpgelu_p_kernel(
                 w2_scale[32 * q : 32 * q + 4, :].bitcast(I32),
                 w2_scales[0][4 * q : 4 * q + 4, :].bitcast(I32),
             )
+
+        nc.sync.dma_start(gates[1][:], gate[:, S // 2 : S])
 
         x_scale = sbuf("x_scale", [P, S], U8)
         nc.vector.tensor_copy(x_scale[:], x_scale_window[:].indirect(offsets[:]))
@@ -163,15 +161,10 @@ def tile_picked_modres_mlpgelu_p_kernel(
                     stop=(g == PASSES - 1 and t == PACK - 1),
                 )
 
-        spread = psum.tile([P, CHUNKS, P], F32, name="spread", tag="y3")
-        for c in range(CHUNKS):
-            nc.tensor.transpose(spread[:, c, :], gate_by_four[:, c : c + 1].to_broadcast([P, P]), identity[:])
         quantise_w1(0)
         for c in range(CHUNKS):
             first_product(0, c, x_word0[:, CHUNK * c : CHUNK * (c + 1)])
         quantise_w1(1)
-        gates = placed("gates", [P, S], F32, 12288)
-        nc.scalar.copy(gates[:].rearrange("p (n c) -> p n c", c=CHUNKS), spread[:].rearrange("p c n -> p n c"))
         first_product(1, 0, x_word1[0][:])
         for c in range(1, CHUNKS):
             gather_x1(c)
@@ -179,54 +172,83 @@ def tile_picked_modres_mlpgelu_p_kernel(
         old_s = [placed("old_s0", [P, 2 * CHUNK], F32, 512)]
         nc.vector.tensor_copy(old_s[0][:], rows_s[:].indirect(entries(0, 2 * CHUNK)))
 
-        gated = sbuf("gated", [P, BLOCKS * S], F32)
-        summed = [sbuf("summed0", [P, 2 * CHUNK], F32), sbuf("summed1", [P, 2 * CHUNK], F32)]
-        for c in range(CHUNKS):
-            cols = slice(CHUNK * c, CHUNK * (c + 1))
+        half = 2 * CHUNK
+        h_word = {}
+        h_scale = {}
+        hs = {}
+
+        def hidden(c):
             if c == 0:
                 h = placed("h0", [P, CHUNK, PACK], BF16, 5120)
-            elif c == 3:
-                h = placed("h3", [P, CHUNK, PACK], BF16, 7168)
-            else:
-                h = sbuf("h%d" % c, [P, CHUNK, PACK], BF16)
-            nc.scalar.activation(h[:], acc[c][:].rearrange("p t n -> p n t"), GELU)
-            if c == 0:
-                h_word = placed("h_word0", [P, CHUNK], U32, 7168)
+                h_word[c] = placed("h_word0", [P, CHUNK], U32, 10240)
             elif c == 1:
-                h_word = placed("h_word1", [P, CHUNK], U32, 8192)
+                h = placed("h1", [P, CHUNK, PACK], BF16, 6144)
+                h_word[c] = placed("h_word1", [P, CHUNK], U32, 8192)
+            elif c == 2:
+                h = sbuf("h2", [P, CHUNK, PACK], BF16)
+                h_word[c] = sbuf("h_word2", [P, CHUNK], U32)
             else:
-                h_word = sbuf("h_word%d" % c, [P, CHUNK], U32)
-            h_scale = sbuf("h_scale%d" % c, [P, CHUNK], U8)
-            nc.vector.quantize_mx(out=h_word[:].bitcast(FP8X4), scales=h_scale[:], in_=h[:].rearrange("p n t -> p (n t)"))
-            y = psum.tile([P, BLOCKS, CHUNK], F32, name="y%d" % c, tag="y%d" % c)
-            for b in range(BLOCKS):
+                h = placed("h3", [P, CHUNK, PACK], BF16, 10240)
+                h_word[c] = sbuf("h_word3", [P, CHUNK], U32)
+            hs[c] = h
+            nc.scalar.activation(h[:], acc[c][:].rearrange("p t n -> p n t"), GELU)
+            h_scale[c] = sbuf("h_scale%d" % c, [P, CHUNK], U8)
+            nc.vector.quantize_mx(
+                out=h_word[c][:].bitcast(FP8X4), scales=h_scale[c][:], in_=h[:].rearrange("p n t -> p (n t)")
+            )
+
+        y = {(b, u): psum.tile([P, half], F32, name="y%d_%d" % (b, u), tag="y%d" % (2 * u + b)) for b in range(BLOCKS) for u in range(2)}
+
+        def second_product(c):
+            for b in (1, 0):
                 nc.tensor.matmul_mx(
-                    out=y[:, b, :],
+                    out=y[b, c // 2][:, CHUNK * (c % 2) : CHUNK * (c % 2 + 1)],
                     lhsT=w2_word[:, 2 * P * b : 2 * P * (b + 1)].bitcast(FP4X4),
                     lhsT_scale=w2_scale[:, P * b : P * (b + 1)],
-                    rhs=h_word[:].bitcast(FP8X4),
-                    rhs_scale=h_scale[:],
+                    rhs=h_word[c][:].bitcast(FP8X4),
+                    rhs_scale=h_scale[c][:],
                     start=True,
                     stop=True,
                 )
-            if c == 0:
-                old_s.append(placed("old_s1", [P, 2 * CHUNK], F32, 5120))
-                nc.vector.tensor_copy(old_s[1][:], rows_s[:].indirect(entries(2 * CHUNK, S)))
-            nc.vector.tensor_tensor(
-                gated[:].rearrange("p (b s) -> p b s", b=BLOCKS)[:, :, cols],
-                y[:],
-                gates[:, cols].unsqueeze(1).to_broadcast([P, BLOCKS, CHUNK]),
-                MULT,
-            )
-            if c % 2 == 1:
-                lo, hi = CHUNK * (c - 1), CHUNK * (c + 1)
-                nc.vector.tensor_tensor(summed[c // 2][:], gated[:, S + lo : S + hi], old_s[c // 2][:], ADD)
 
-        old_v = placed("old_v", [P, S], F32, 8192)
-        nc.scalar.activation(old_v[:], rows_v[:].indirect(offsets[:]), COPY)
-        for lo in range(0, S, 2 * CHUNK):
-            nc.scalar.activation(rows_s[:].indirect(entries(lo, lo + 2 * CHUNK)), summed[lo // (2 * CHUNK)][:], COPY)
+        gated_v = sbuf("gated_v", [P, S], F32)
+        gated_s = [sbuf("gated_s%d" % u, [P, half], F32) for u in range(2)]
+        summed = {1: sbuf("summed1", [P, half], F32)}
+
+        def gate_product(b, u):
+            cols = slice(half * u, half * (u + 1))
+            nc.vector.tensor_tensor(gated_v[:, cols] if b == 0 else gated_s[u][:], y[b, u][:], gates[u][:], MULT)
+
+        hidden(0)
+        old_s.append(placed("old_s2", [P, CHUNK], F32, 5120))
+        nc.vector.tensor_copy(old_s[1][:], rows_s[:].indirect(entries(half, 3 * CHUNK)))
+        hidden(1)
+        old_s.append(placed("old_s3", [P, CHUNK], F32, 6144))
+        nc.vector.tensor_copy(old_s[2][:], rows_s[:].indirect(entries(3 * CHUNK, S)))
+        hidden(2)
+        second_product(0)
+        second_product(1)
+        gate_product(1, 0)
+        gate_product(0, 0)
+        summed[0] = sbuf("summed0", [P, half], F32)
+        nc.vector.tensor_tensor(summed[0][:], gated_s[0][:], old_s[0][:], ADD)
+        hidden(3)
+        old_v = [placed("old_v0", [P, OLD_ON_VECTOR], F32, 10240)]
+        nc.vector.tensor_copy(old_v[0][:], rows_v[:].indirect(entries(0, OLD_ON_VECTOR)))
+        second_product(2)
+        second_product(3)
+        gate_product(1, 1)
+        gate_product(0, 1)
+        for i in range(2):
+            cols = slice(CHUNK * i, CHUNK * (i + 1))
+            nc.vector.tensor_tensor(summed[1][:, cols], gated_s[1][:, cols], old_s[1 + i][:], ADD)
+
+        old_v.append(placed("old_v1", [P, S - OLD_ON_VECTOR], F32, 8192))
+        nc.scalar.activation(old_v[1][:], rows_v[:].indirect(entries(OLD_ON_VECTOR, S)), COPY)
+        for u in range(2):
+            nc.scalar.activation(rows_s[:].indirect(entries(half * u, half * (u + 1))), summed[u][:], COPY)
         nc.sync.dma_start(out[P : 2 * P, :], rows_s[:])
 
-        nc.vector.tensor_tensor(rows_v[:].indirect(offsets[:]), gated[:, 0:S], old_v[:], ADD)
+        for i, lo, hi in ((1, OLD_ON_VECTOR, S), (0, 0, OLD_ON_VECTOR)):
+            nc.vector.tensor_tensor(rows_v[:].indirect(entries(lo, hi)), gated_v[:, lo:hi], old_v[i][:], ADD)
         nc.sync.dma_start(out[0:P, :], rows_v[:])

@@ -166,9 +166,12 @@ def tile_picked_modres_mlpgelu_p_kernel(
             first_product(0, c, x_word0[:, CHUNK * c : CHUNK * (c + 1)])
         quantise_w1(1)
         first_product(1, 0, x_word1[0][:])
-        for c in range(1, CHUNKS):
-            gather_x1(c)
-            first_product(1, c, x_word1[c][:])
+        gather_x1(1)
+        first_product(1, 1, x_word1[1][:])
+        x_word1_last = placed("x_word1_last", [P, 2 * CHUNK], U32, 2048)
+        nc.vector.tensor_copy(x_word1_last[:], x_word_window[1][:].indirect(entries(2 * CHUNK, S)))
+        for c in range(2, CHUNKS):
+            first_product(1, c, x_word1_last[:, CHUNK * (c - 2) : CHUNK * (c - 1)])
         old_s = [placed("old_s0", [P, 2 * CHUNK], F32, 512)]
         nc.vector.tensor_copy(old_s[0][:], rows_s[:].indirect(entries(0, 2 * CHUNK)))
 
@@ -233,22 +236,20 @@ def tile_picked_modres_mlpgelu_p_kernel(
         summed[0] = sbuf("summed0", [P, half], F32)
         nc.vector.tensor_tensor(summed[0][:], gated_s[0][:], old_s[0][:], ADD)
         hidden(3)
-        old_v = [placed("old_v0", [P, OLD_ON_VECTOR], F32, 10240)]
-        nc.vector.tensor_copy(old_v[0][:], rows_v[:].indirect(entries(0, OLD_ON_VECTOR)))
         second_product(2)
         second_product(3)
+        old_v = placed("old_v", [P, S], F32, 8192)
+        nc.vector.tensor_copy(old_v[:, 0:OLD_ON_VECTOR], rows_v[:].indirect(entries(0, OLD_ON_VECTOR)))
         gate_product(1, 1)
         gate_product(0, 1)
         for i in range(2):
             cols = slice(CHUNK * i, CHUNK * (i + 1))
             nc.vector.tensor_tensor(summed[1][:, cols], gated_s[1][:, cols], old_s[1 + i][:], ADD)
 
-        old_v.append(placed("old_v1", [P, S - OLD_ON_VECTOR], F32, 8192))
-        nc.scalar.activation(old_v[1][:], rows_v[:].indirect(entries(OLD_ON_VECTOR, S)), COPY)
+        nc.scalar.activation(old_v[:, OLD_ON_VECTOR:S], rows_v[:].indirect(entries(OLD_ON_VECTOR, S)), COPY)
         for u in range(2):
             nc.scalar.activation(rows_s[:].indirect(entries(half * u, half * (u + 1))), summed[u][:], COPY)
         nc.sync.dma_start(out[P : 2 * P, :], rows_s[:])
 
-        for i, lo, hi in ((1, OLD_ON_VECTOR, S), (0, 0, OLD_ON_VECTOR)):
-            nc.vector.tensor_tensor(rows_v[:].indirect(entries(lo, hi)), gated_v[:, lo:hi], old_v[i][:], ADD)
+        nc.vector.tensor_tensor(rows_v[:].indirect(offsets[:]), gated_v[:], old_v[:], ADD)
         nc.sync.dma_start(out[0:P, :], rows_v[:])

@@ -27,7 +27,6 @@ ADD = mybir.AluOpType.add
 MULT = mybir.AluOpType.mult
 
 EXTRA_ON_VECTOR = (0, 0)
-OLD_ON_VECTOR = 192
 
 
 def tile_picked_modres_mlpgelu_p_kernel(
@@ -87,10 +86,10 @@ def tile_picked_modres_mlpgelu_p_kernel(
             nc.sync.dma_start(w1_raw[g][:], w1_rows[g])
         load_x_words(1)
 
-        rows_s = sbuf("rows_s", [P, T], F32)
-        nc.sync.dma_start(rows_s[:], res[P : 2 * P, :])
         rows_v = sbuf("rows_v", [P, T], F32)
         nc.sync.dma_start(rows_v[:], res[0:P, :])
+        rows_read = sbuf("rows_read", [P, T], F32)
+        nc.sync.dma_start(rows_read[:], res[P : 2 * P, :])
         gates = [sbuf("gates%d" % u, [P, S // 2], F32) for u in range(2)]
         nc.sync.dma_start(gates[0][:], gate[:, 0 : S // 2])
         w2_word = sbuf("w2_word", [P, 2 * N], U8)
@@ -100,7 +99,8 @@ def tile_picked_modres_mlpgelu_p_kernel(
                 w2_scale[32 * q : 32 * q + 4, :].bitcast(I32),
                 w2_scales[0][4 * q : 4 * q + 4, :].bitcast(I32),
             )
-
+        rows_s = sbuf("rows_s", [P, T], F32)
+        nc.sync.dma_start(rows_s[:], res[P : 2 * P, :])
         nc.sync.dma_start(gates[1][:], gate[:, S // 2 : S])
 
         x_scale = sbuf("x_scale", [P, S], U8)
@@ -118,7 +118,7 @@ def tile_picked_modres_mlpgelu_p_kernel(
             if c == 0:
                 x_word1[c] = sbuf("x_word1_0", [P, CHUNK], U32)
             else:
-                x_word1[c] = placed("x_word1_%d" % c, [P, CHUNK], U32, 1024 + 512 * c)
+                x_word1[c] = placed("x_word1_%d" % c, [P, CHUNK], U32, 2560)
             nc.vector.tensor_copy(x_word1[c][:], x_word_window[1][:].indirect(entries(CHUNK * c, CHUNK * (c + 1))))
 
         def quantise_w1(g):
@@ -127,7 +127,7 @@ def tile_picked_modres_mlpgelu_p_kernel(
             if g == 0:
                 rounded.append(sbuf("w1_bf16_0_1", [P, 2, P, PACK], BF16))
             else:
-                rounded.append(placed("w1_bf16_1_1", [P, 2, P, PACK], BF16, 1024))
+                rounded.append(placed("w1_bf16_1_1", [P, 2, P, PACK], BF16, 2048))
             dst = [rounded[u][:].rearrange("p t m j -> p m j t") for u in range(2)]
             nc.vector.tensor_copy(dst[0], src[:, :, :, 0:2])
             extra = EXTRA_ON_VECTOR[g]
@@ -168,44 +168,46 @@ def tile_picked_modres_mlpgelu_p_kernel(
         first_product(1, 0, x_word1[0][:])
         gather_x1(1)
         first_product(1, 1, x_word1[1][:])
-        x_word1_last = placed("x_word1_last", [P, 2 * CHUNK], U32, 2048)
+        x_word1_last = placed("x_word1_last", [P, 2 * CHUNK], U32, 3072)
         nc.vector.tensor_copy(x_word1_last[:], x_word_window[1][:].indirect(entries(2 * CHUNK, S)))
         for c in range(2, CHUNKS):
             first_product(1, c, x_word1_last[:, CHUNK * (c - 2) : CHUNK * (c - 1)])
-        old_s = [placed("old_s0", [P, 2 * CHUNK], F32, 512)]
-        nc.vector.tensor_copy(old_s[0][:], rows_s[:].indirect(entries(0, 2 * CHUNK)))
+        old_v = placed("old_v", [P, S], F32, 512)
+
+        def gather_old_v(lo, hi):
+            nc.vector.tensor_copy(old_v[:, lo:hi], rows_v[:].indirect(entries(lo, hi)))
+
+        gather_old_v(0, CHUNK)
 
         half = 2 * CHUNK
         h_word = {}
         h_scale = {}
-        hs = {}
 
         def hidden(c):
-            if c == 0:
-                h = placed("h0", [P, CHUNK, PACK], BF16, 5120)
-                h_word[c] = placed("h_word0", [P, CHUNK], U32, 10240)
-            elif c == 1:
-                h = placed("h1", [P, CHUNK, PACK], BF16, 6144)
-                h_word[c] = placed("h_word1", [P, CHUNK], U32, 8192)
-            elif c == 2:
-                h = sbuf("h2", [P, CHUNK, PACK], BF16)
-                h_word[c] = sbuf("h_word2", [P, CHUNK], U32)
+            if c == 2:
+                h = old_v[:, CHUNK : 3 * CHUNK].bitcast(BF16)
             else:
-                h = placed("h3", [P, CHUNK, PACK], BF16, 10240)
-                h_word[c] = sbuf("h_word3", [P, CHUNK], U32)
-            hs[c] = h
-            nc.scalar.activation(h[:], acc[c][:].rearrange("p t n -> p n t"), GELU)
+                h = sbuf("h%d" % c, [P, CHUNK * PACK], BF16)[:]
+            h_word[c] = placed("h_word%d" % c, [P, CHUNK], U32, 8192 + 512 * (c % 2))
+            nc.scalar.activation(h.rearrange("p (n t) -> p n t", t=PACK), acc[c][:].rearrange("p t n -> p n t"), GELU)
             h_scale[c] = sbuf("h_scale%d" % c, [P, CHUNK], U8)
-            nc.vector.quantize_mx(
-                out=h_word[c][:].bitcast(FP8X4), scales=h_scale[c][:], in_=h[:].rearrange("p n t -> p (n t)")
-            )
+            nc.vector.quantize_mx(out=h_word[c][:].bitcast(FP8X4), scales=h_scale[c][:], in_=h)
 
-        y = {(b, u): psum.tile([P, half], F32, name="y%d_%d" % (b, u), tag="y%d" % (2 * u + b)) for b in range(BLOCKS) for u in range(2)}
+        y_v = [psum.tile([P, half], F32, name="y_v%d" % u, tag="y_v%d" % u) for u in range(2)]
+        y_late = psum.tile([P, half], F32, name="y_late", tag="y_late")
+        y_s = {}
 
         def second_product(c):
+            cols = slice(CHUNK * (c % 2), CHUNK * (c % 2 + 1))
+            if c == 0:
+                y_s[c] = psum.tile([P, CHUNK], F32, name="y_s0", tag="acc0")[:]
+            elif c == 1:
+                y_s[c] = psum.tile([P, CHUNK], F32, name="y_s1", tag="y_s1")[:]
+            else:
+                y_s[c] = y_late[:, cols]
             for b in (1, 0):
                 nc.tensor.matmul_mx(
-                    out=y[b, c // 2][:, CHUNK * (c % 2) : CHUNK * (c % 2 + 1)],
+                    out=y_s[c] if b == 1 else y_v[c // 2][:, cols],
                     lhsT=w2_word[:, 2 * P * b : 2 * P * (b + 1)].bitcast(FP4X4),
                     lhsT_scale=w2_scale[:, P * b : P * (b + 1)],
                     rhs=h_word[c][:].bitcast(FP8X4),
@@ -216,40 +218,38 @@ def tile_picked_modres_mlpgelu_p_kernel(
 
         gated_v = sbuf("gated_v", [P, S], F32)
         gated_s = [sbuf("gated_s%d" % u, [P, half], F32) for u in range(2)]
-        summed = {1: sbuf("summed1", [P, half], F32)}
+        summed = [sbuf("summed%d" % u, [P, half], F32) for u in range(2)]
 
-        def gate_product(b, u):
-            cols = slice(half * u, half * (u + 1))
-            nc.vector.tensor_tensor(gated_v[:, cols] if b == 0 else gated_s[u][:], y[b, u][:], gates[u][:], MULT)
+        def gate_early(c):
+            cols = slice(CHUNK * c, CHUNK * (c + 1))
+            nc.vector.tensor_tensor(gated_s[0][:, cols], y_s[c], gates[0][:, cols], MULT)
+
+        def sum_early(c):
+            cols = slice(CHUNK * c, CHUNK * (c + 1))
+            window = rows_read[:].indirect(entries(CHUNK * c, CHUNK * (c + 1)))
+            nc.vector.tensor_tensor(summed[0][:, cols], window, gated_s[0][:, cols], ADD)
 
         hidden(0)
-        old_s.append(placed("old_s2", [P, CHUNK], F32, 5120))
-        nc.vector.tensor_copy(old_s[1][:], rows_s[:].indirect(entries(half, 3 * CHUNK)))
         hidden(1)
-        old_s.append(placed("old_s3", [P, CHUNK], F32, 6144))
-        nc.vector.tensor_copy(old_s[2][:], rows_s[:].indirect(entries(3 * CHUNK, S)))
-        hidden(2)
         second_product(0)
         second_product(1)
-        gate_product(1, 0)
-        gate_product(0, 0)
-        summed[0] = sbuf("summed0", [P, half], F32)
-        nc.vector.tensor_tensor(summed[0][:], gated_s[0][:], old_s[0][:], ADD)
+        gate_early(0)
+        hidden(2)
+        sum_early(0)
+        gate_early(1)
         hidden(3)
+        sum_early(1)
+        nc.vector.tensor_tensor(gated_v[:, 0:half], y_v[0][:], gates[0][:], MULT)
         second_product(2)
         second_product(3)
-        old_v = placed("old_v", [P, S], F32, 8192)
-        nc.vector.tensor_copy(old_v[:, 0:OLD_ON_VECTOR], rows_v[:].indirect(entries(0, OLD_ON_VECTOR)))
-        gate_product(1, 1)
-        gate_product(0, 1)
-        for i in range(2):
-            cols = slice(CHUNK * i, CHUNK * (i + 1))
-            nc.vector.tensor_tensor(summed[1][:, cols], gated_s[1][:, cols], old_s[1 + i][:], ADD)
+        nc.vector.tensor_tensor(gated_s[1][:], y_late[:], gates[1][:], MULT)
+        nc.vector.tensor_tensor(gated_v[:, half:S], y_v[1][:], gates[1][:], MULT)
+        nc.vector.tensor_tensor(summed[1][:], rows_read[:].indirect(entries(half, S)), gated_s[1][:], ADD)
 
-        nc.scalar.activation(old_v[:, OLD_ON_VECTOR:S], rows_v[:].indirect(entries(OLD_ON_VECTOR, S)), COPY)
+        nc.scalar.activation(old_v[:, CHUNK:S], rows_v[:].indirect(entries(CHUNK, S)), COPY)
         for u in range(2):
             nc.scalar.activation(rows_s[:].indirect(entries(half * u, half * (u + 1))), summed[u][:], COPY)
-        nc.sync.dma_start(out[P : 2 * P, :], rows_s[:])
+        nc.scalar.dma_start(out[P : 2 * P, :], rows_s[:])
 
         nc.vector.tensor_tensor(rows_v[:].indirect(offsets[:]), gated_v[:], old_v[:], ADD)
         nc.sync.dma_start(out[0:P, :], rows_v[:])

@@ -7,11 +7,10 @@ FLOPS = 2 * S * (K * H + H * N)
 
 P = 128
 PACK = 4
-PASSES = K // (P * PACK)
 QUADRANTS = 4
-BLOCKS = N // P
 CHUNK = 128
 CHUNKS = S // CHUNK
+HALF = S // 2
 
 F32 = mybir.dt.float32
 BF16 = mybir.dt.bfloat16
@@ -26,8 +25,6 @@ COPY = mybir.ActivationFunctionType.Copy
 ADD = mybir.AluOpType.add
 MULT = mybir.AluOpType.mult
 
-EXTRA_ON_VECTOR = (0, 0)
-
 
 def tile_picked_modres_mlpgelu_p_kernel(
     tc, x_words, x_scales, gate, res, w1, w2_words, w2_scales, offs, out
@@ -35,25 +32,23 @@ def tile_picked_modres_mlpgelu_p_kernel(
     nc = tc.nc
     with ExitStack() as ctx:
         keep = ctx.enter_context(tc.tile_pool(name="keep", bufs=1))
-        shared = ctx.enter_context(tc.tile_pool(name="shared", bufs=1))
         by_hand = ctx.enter_context(tc.tile_pool(name="by_hand", bufs=1))
         psum = ctx.enter_context(tc.psum_pool(name="psum", bufs=1))
 
         def sbuf(name, shape, dtype):
-            return keep.tile(shape, dtype, name=name, align_bytes=64)
-
-        def reused(name, shape, dtype, tag):
-            return shared.tile(shape, dtype, name=name, tag=tag, align_bytes=64)
+            return keep.tile(shape, dtype, name=name, align_bytes=256)
 
         def placed(name, shape, dtype, offset):
             return by_hand.tile(shape, dtype, name=name, offset=offset, align_bytes=64)
 
-        x_scale_window = reused("x_scale_window", [P, T], U8, "scale_window")
+        SPLIT0 = 72
+        OLD_V = 256
+        x_scale_window = sbuf("x_scale_window", [P, T], U8)
         nc.gpsimd.memset(x_scale_window[:].bitcast(I32), 0)
 
         def load_x_scales(queue, q):
             queue.dma_start(
-                x_scale_window[32 * q : 32 * q + 4 * PASSES, :].bitcast(I32),
+                x_scale_window[32 * q : 32 * q + 8, :].bitcast(I32),
                 x_scales[:, 4 * q : 4 * q + 4, :].bitcast(I32),
             )
 
@@ -71,27 +66,29 @@ def tile_picked_modres_mlpgelu_p_kernel(
         def entries(lo, hi):
             return offsets[:, lo // 16 : hi // 16]
 
-        x_word_window = [sbuf("x_word_window%d" % g, [P, T], U32) for g in range(PASSES)]
+        x_window = [sbuf("x_window%d" % g, [P, T], U32) for g in range(2)]
 
         def load_x_words(g):
-            nc.sync.dma_start(x_word_window[g][:].bitcast(I32), x_words[g].rearrange("p n j -> p (n j)").bitcast(I32))
+            nc.sync.dma_start(x_window[g][:].bitcast(I32), x_words[g].rearrange("p n j -> p (n j)").bitcast(I32))
 
         load_x_words(0)
         nc.sync.dma_start(offsets[:], offs)
         for q in range(2, QUADRANTS):
             load_x_scales(nc.sync, q)
-        w1_rows = w1.rearrange("(g p j) c -> g p j c", g=PASSES, j=PACK)
-        w1_raw = [sbuf("w1_raw%d" % g, [P, PACK, H], F32) for g in range(PASSES)]
-        for g in range(PASSES):
-            nc.sync.dma_start(w1_raw[g][:], w1_rows[g])
+        w1_rows = w1.rearrange("(g p j) c -> g p j c", g=2, j=PACK)
+        w1_first = sbuf("w1_first", [P, PACK, H], F32)
+        nc.sync.dma_start(w1_first[:], w1_rows[0])
+        w1_last = [sbuf("w1_last%d" % h, [P, PACK, H // 2], F32) for h in range(2)]
+        for h in range(2):
+            nc.sync.dma_start(w1_last[h][:], w1_rows[1][:, :, H // 2 * h : H // 2 * (h + 1)])
         load_x_words(1)
 
         rows_v = sbuf("rows_v", [P, T], F32)
         nc.sync.dma_start(rows_v[:], res[0:P, :])
         rows_read = sbuf("rows_read", [P, T], F32)
         nc.sync.dma_start(rows_read[:], res[P : 2 * P, :])
-        gates = [sbuf("gates%d" % u, [P, S // 2], F32) for u in range(2)]
-        nc.sync.dma_start(gates[0][:], gate[:, 0 : S // 2])
+        gates = [sbuf("gates%d" % u, [P, HALF], F32) for u in range(2)]
+        nc.sync.dma_start(gates[0][:], gate[:, 0:HALF])
         w2_word = sbuf("w2_word", [P, 2 * N], U8)
         nc.sync.dma_start(w2_word[:].bitcast(I32), w2_words[0].bitcast(I32))
         for q in range(QUADRANTS):
@@ -101,51 +98,42 @@ def tile_picked_modres_mlpgelu_p_kernel(
             )
         rows_s = sbuf("rows_s", [P, T], F32)
         nc.sync.dma_start(rows_s[:], res[P : 2 * P, :])
-        nc.sync.dma_start(gates[1][:], gate[:, S // 2 : S])
+        nc.sync.dma_start(gates[1][:], gate[:, HALF:S])
 
         x_scale = sbuf("x_scale", [P, S], U8)
         nc.vector.tensor_copy(x_scale[:], x_scale_window[:].indirect(offsets[:]))
         x_word0 = sbuf("x_word0", [P, S], U32)
-        nc.vector.tensor_copy(x_word0[:], x_word_window[0][:].indirect(offsets[:]))
+        nc.vector.tensor_copy(x_word0[:], x_window[0][:].indirect(offsets[:]))
 
         acc = [psum.tile([P, PACK, CHUNK], F32, name="acc%d" % c, tag="acc%d" % c) for c in range(CHUNKS)]
         w1_word = {}
         w1_scale = {}
-
-        x_word1 = {}
-
-        def gather_x1(c):
-            if c == 0:
-                x_word1[c] = sbuf("x_word1_0", [P, CHUNK], U32)
-            else:
-                x_word1[c] = placed("x_word1_%d" % c, [P, CHUNK], U32, 2560)
-            nc.vector.tensor_copy(x_word1[c][:], x_word_window[1][:].indirect(entries(CHUNK * c, CHUNK * (c + 1))))
-
-        def quantise_w1(g):
-            src = w1_raw[g][:].rearrange("p j (m t) -> p m j t", t=PACK)
-            rounded = [sbuf("w1_bf16_%d_0" % g, [P, 2, P, PACK], BF16)]
-            if g == 0:
-                rounded.append(sbuf("w1_bf16_0_1", [P, 2, P, PACK], BF16))
-            else:
-                rounded.append(placed("w1_bf16_1_1", [P, 2, P, PACK], BF16, 2048))
-            dst = [rounded[u][:].rearrange("p t m j -> p m j t") for u in range(2)]
-            nc.vector.tensor_copy(dst[0], src[:, :, :, 0:2])
-            extra = EXTRA_ON_VECTOR[g]
-            if extra > 0:
-                nc.vector.tensor_copy(dst[1][:, 0:extra], src[:, 0:extra, :, 2:4])
-            nc.scalar.copy(dst[1][:, extra:P], src[:, extra:P, :, 2:4])
+        for g in range(2):
             for u in range(2):
-                if (g, u) == (1, 1):
-                    gather_x1(0)
                 w1_word[g, u] = sbuf("w1_word%d_%d" % (g, u), [P, 2 * P], U32)
-                if (g, u) == (0, 0):
-                    w1_scale[g, u] = reused("w1_scale0_0", [P, 2 * P], U8, "scale_window")
-                else:
-                    w1_scale[g, u] = sbuf("w1_scale%d_%d" % (g, u), [P, 2 * P], U8)
+                w1_scale[g, u] = sbuf("w1_scale%d_%d" % (g, u), [P, 2 * P], U8)
+
+        def round_pairs(name, raw, units):
+            src = raw[:].rearrange("p j (m t) -> p m j t", t=PACK)
+            pairs = [sbuf("%s_%d" % (name, u), [P, 2, units, PACK], BF16) for u in range(2)]
+            nc.vector.tensor_copy(pairs[0][:].rearrange("p t m j -> p m j t"), src[:, :, :, 0:2])
+            nc.scalar.copy(pairs[1][:].rearrange("p t m j -> p m j t"), src[:, :, :, 2:4])
+            return pairs
+
+        def quantise_first(u, pairs):
+            nc.vector.quantize_mx(
+                out=w1_word[0, u][:].bitcast(FP8X4),
+                scales=w1_scale[0, u][:],
+                in_=pairs[u][:].rearrange("p t m j -> p (t m j)"),
+            )
+
+        def quantise_last(h, u, pairs):
+            for t in range(2):
+                cols = slice(P * t + 64 * h, P * t + 64 * (h + 1))
                 nc.vector.quantize_mx(
-                    out=w1_word[g, u][:].bitcast(FP8X4),
-                    scales=w1_scale[g, u][:],
-                    in_=rounded[u][:].rearrange("p t m j -> p (t m j)"),
+                    out=w1_word[1, u][:, cols].bitcast(FP8X4),
+                    scales=w1_scale[1, u][:, cols],
+                    in_=pairs[u][:, t].rearrange("p m j -> p (m j)"),
                 )
 
         def first_product(g, c, words):
@@ -158,43 +146,62 @@ def tile_picked_modres_mlpgelu_p_kernel(
                     rhs=words.bitcast(FP8X4),
                     rhs_scale=x_scale[4 * g : P, CHUNK * c : CHUNK * (c + 1)],
                     start=(g == 0 and t == 0),
-                    stop=(g == PASSES - 1 and t == PACK - 1),
+                    stop=(g == 1 and t == PACK - 1),
                 )
 
-        quantise_w1(0)
+        src = w1_first[:].rearrange("p j (m t) -> p m j t", t=PACK)
+        first = [sbuf("w1_bf16_first_%d" % u, [P, 2, P, PACK], BF16) for u in range(2)]
+        dst = [first[u][:].rearrange("p t m j -> p m j t") for u in range(2)]
+        nc.vector.tensor_copy(dst[0][:, 0:SPLIT0], src[:, 0:SPLIT0, :, 0:2])
+        nc.scalar.copy(dst[0][:, SPLIT0:P], src[:, SPLIT0:P, :, 0:2])
+        for t in range(2):
+            nc.vector.quantize_mx(
+                out=w1_word[0, 0][:, P * t : P * (t + 1)].bitcast(FP8X4),
+                scales=w1_scale[0, 0][:, P * t : P * (t + 1)],
+                in_=first[0][:, t].rearrange("p m j -> p (m j)"),
+            )
+        nc.scalar.copy(dst[1], src[:, :, :, 2:4])
+        early = sbuf("w1_bf16_early", [P, PACK, 64, PACK], BF16)
+        nc.vector.tensor_copy(
+            early[:].rearrange("p t m j -> p m j t"), w1_last[0][:].rearrange("p j (m t) -> p m j t", t=PACK)
+        )
+        last0 = [early[:, 0:2], early[:, 2:4]]
+        quantise_first(1, first)
         for c in range(CHUNKS):
             first_product(0, c, x_word0[:, CHUNK * c : CHUNK * (c + 1)])
-        quantise_w1(1)
+        quantise_last(0, 0, last0)
+        last1 = round_pairs("w1_bf16_last1", w1_last[1], 64)
+        quantise_last(0, 1, last0)
+        quantise_last(1, 0, last1)
+        quantise_last(1, 1, last1)
+
+        x_word1 = [sbuf("x_word1_%d" % i, [P, n], U32) for i, n in enumerate((CHUNK, CHUNK, HALF))]
+        nc.vector.tensor_copy(x_word1[0][:], x_window[1][:].indirect(entries(0, CHUNK)))
         first_product(1, 0, x_word1[0][:])
-        gather_x1(1)
+        nc.vector.tensor_copy(x_word1[1][:], x_window[1][:].indirect(entries(CHUNK, HALF)))
         first_product(1, 1, x_word1[1][:])
-        x_word1_last = placed("x_word1_last", [P, 2 * CHUNK], U32, 3072)
-        nc.vector.tensor_copy(x_word1_last[:], x_word_window[1][:].indirect(entries(2 * CHUNK, S)))
+        nc.vector.tensor_copy(x_word1[2][:], x_window[1][:].indirect(entries(HALF, S)))
         for c in range(2, CHUNKS):
-            first_product(1, c, x_word1_last[:, CHUNK * (c - 2) : CHUNK * (c - 1)])
-        old_v = placed("old_v", [P, S], F32, 512)
+            first_product(1, c, x_word1[2][:, CHUNK * (c - 2) : CHUNK * (c - 1)])
 
-        def gather_old_v(lo, hi):
-            nc.vector.tensor_copy(old_v[:, lo:hi], rows_v[:].indirect(entries(lo, hi)))
-
-        gather_old_v(0, CHUNK)
-
-        half = 2 * CHUNK
+        old_v = sbuf("old_v", [P, max(S, OLD_V + HALF)], F32)
+        nc.vector.tensor_copy(old_v[:, 0:OLD_V], rows_v[:].indirect(entries(0, OLD_V)))
         h_word = {}
         h_scale = {}
+        h = {}
 
         def hidden(c):
             if c == 2:
-                h = old_v[:, CHUNK : 3 * CHUNK].bitcast(BF16)
+                h[c] = old_v[:, OLD_V : OLD_V + HALF].bitcast(BF16)
             else:
-                h = sbuf("h%d" % c, [P, CHUNK * PACK], BF16)[:]
-            h_word[c] = placed("h_word%d" % c, [P, CHUNK], U32, 8192 + 512 * (c % 2))
-            nc.scalar.activation(h.rearrange("p (n t) -> p n t", t=PACK), acc[c][:].rearrange("p t n -> p n t"), GELU)
+                h[c] = sbuf("h%d" % c, [P, CHUNK * PACK], BF16)[:]
+            nc.scalar.activation(h[c].rearrange("p (n t) -> p n t", t=PACK), acc[c][:].rearrange("p t n -> p n t"), GELU)
+            h_word[c] = placed("h_word%d" % c, [P, CHUNK], U32, 512 * (c % 2))
             h_scale[c] = sbuf("h_scale%d" % c, [P, CHUNK], U8)
-            nc.vector.quantize_mx(out=h_word[c][:].bitcast(FP8X4), scales=h_scale[c][:], in_=h)
+            nc.vector.quantize_mx(out=h_word[c][:].bitcast(FP8X4), scales=h_scale[c][:], in_=h[c])
 
-        y_v = [psum.tile([P, half], F32, name="y_v%d" % u, tag="y_v%d" % u) for u in range(2)]
-        y_late = psum.tile([P, half], F32, name="y_late", tag="y_late")
+        y_v = [psum.tile([P, HALF], F32, name="y_v%d" % u, tag="y_v%d" % u) for u in range(2)]
+        y_late = psum.tile([P, HALF], F32, name="y_late", tag="y_late")
         y_s = {}
 
         def second_product(c):
@@ -217,8 +224,8 @@ def tile_picked_modres_mlpgelu_p_kernel(
                 )
 
         gated_v = sbuf("gated_v", [P, S], F32)
-        gated_s = [sbuf("gated_s%d" % u, [P, half], F32) for u in range(2)]
-        summed = [sbuf("summed%d" % u, [P, half], F32) for u in range(2)]
+        gated_s = [sbuf("gated_s%d" % u, [P, HALF], F32) for u in range(2)]
+        summed = [sbuf("summed%d" % u, [P, HALF], F32) for u in range(2)]
 
         def gate_early(c):
             cols = slice(CHUNK * c, CHUNK * (c + 1))
@@ -239,17 +246,17 @@ def tile_picked_modres_mlpgelu_p_kernel(
         gate_early(1)
         hidden(3)
         sum_early(1)
-        nc.vector.tensor_tensor(gated_v[:, 0:half], y_v[0][:], gates[0][:], MULT)
+        nc.vector.tensor_tensor(gated_v[:, 0:HALF], y_v[0][:], gates[0][:], MULT)
         second_product(2)
         second_product(3)
         nc.vector.tensor_tensor(gated_s[1][:], y_late[:], gates[1][:], MULT)
-        nc.vector.tensor_tensor(gated_v[:, half:S], y_v[1][:], gates[1][:], MULT)
-        nc.vector.tensor_tensor(summed[1][:], rows_read[:].indirect(entries(half, S)), gated_s[1][:], ADD)
+        nc.vector.tensor_tensor(gated_v[:, HALF:S], y_v[1][:], gates[1][:], MULT)
+        nc.vector.tensor_tensor(summed[1][:], rows_read[:].indirect(entries(HALF, S)), gated_s[1][:], ADD)
 
-        nc.scalar.activation(old_v[:, CHUNK:S], rows_v[:].indirect(entries(CHUNK, S)), COPY)
+        nc.scalar.activation(old_v[:, OLD_V:S], rows_v[:].indirect(entries(OLD_V, S)), COPY)
         for u in range(2):
-            nc.scalar.activation(rows_s[:].indirect(entries(half * u, half * (u + 1))), summed[u][:], COPY)
+            nc.scalar.activation(rows_s[:].indirect(entries(HALF * u, HALF * (u + 1))), summed[u][:], COPY)
         nc.scalar.dma_start(out[P : 2 * P, :], rows_s[:])
 
-        nc.vector.tensor_tensor(rows_v[:].indirect(offsets[:]), gated_v[:], old_v[:], ADD)
+        nc.vector.tensor_tensor(rows_v[:].indirect(offsets[:]), gated_v[:], old_v[:, 0:S], ADD)
         nc.sync.dma_start(out[0:P, :], rows_v[:])

@@ -41,8 +41,7 @@ def tile_picked_modres_mlpgelu_p_kernel(
         def placed(name, shape, dtype, offset):
             return by_hand.tile(shape, dtype, name=name, offset=offset, align_bytes=64)
 
-        SPLIT0 = 72
-        OLD_V = 256
+        OLD_V = 128
         x_scale_window = sbuf("x_scale_window", [P, T], U8)
         nc.gpsimd.memset(x_scale_window[:].bitcast(I32), 0)
 
@@ -149,23 +148,9 @@ def tile_picked_modres_mlpgelu_p_kernel(
                     stop=(g == 1 and t == PACK - 1),
                 )
 
-        src = w1_first[:].rearrange("p j (m t) -> p m j t", t=PACK)
-        first = [sbuf("w1_bf16_first_%d" % u, [P, 2, P, PACK], BF16) for u in range(2)]
-        dst = [first[u][:].rearrange("p t m j -> p m j t") for u in range(2)]
-        nc.vector.tensor_copy(dst[0][:, 0:SPLIT0], src[:, 0:SPLIT0, :, 0:2])
-        nc.scalar.copy(dst[0][:, SPLIT0:P], src[:, SPLIT0:P, :, 0:2])
-        for t in range(2):
-            nc.vector.quantize_mx(
-                out=w1_word[0, 0][:, P * t : P * (t + 1)].bitcast(FP8X4),
-                scales=w1_scale[0, 0][:, P * t : P * (t + 1)],
-                in_=first[0][:, t].rearrange("p m j -> p (m j)"),
-            )
-        nc.scalar.copy(dst[1], src[:, :, :, 2:4])
-        early = sbuf("w1_bf16_early", [P, PACK, 64, PACK], BF16)
-        nc.vector.tensor_copy(
-            early[:].rearrange("p t m j -> p m j t"), w1_last[0][:].rearrange("p j (m t) -> p m j t", t=PACK)
-        )
-        last0 = [early[:, 0:2], early[:, 2:4]]
+        first = round_pairs("w1_bf16_first", w1_first, P)
+        quantise_first(0, first)
+        last0 = round_pairs("w1_bf16_last0", w1_last[0], 64)
         quantise_first(1, first)
         for c in range(CHUNKS):
             first_product(0, c, x_word0[:, CHUNK * c : CHUNK * (c + 1)])

@@ -41,7 +41,7 @@ def tile_picked_modres_mlpgelu_p_kernel(
         def placed(name, shape, dtype, offset):
             return by_hand.tile(shape, dtype, name=name, offset=offset, align_bytes=64)
 
-        OLD_V = 128
+        OLD_V = 192
         x_scale_window = sbuf("x_scale_window", [P, T], U8)
         nc.gpsimd.memset(x_scale_window[:].bitcast(I32), 0)
 
@@ -171,71 +171,55 @@ def tile_picked_modres_mlpgelu_p_kernel(
 
         old_v = sbuf("old_v", [P, max(S, OLD_V + HALF)], F32)
         nc.vector.tensor_copy(old_v[:, 0:OLD_V], rows_v[:].indirect(entries(0, OLD_V)))
-        h_word = {}
-        h_scale = {}
-        h = {}
+        def gelu(c, h):
+            nc.scalar.activation(h.rearrange("p (n t) -> p n t", t=PACK), acc[c][:].rearrange("p t n -> p n t"), GELU)
 
-        def hidden(c):
-            if c == 2:
-                h[c] = old_v[:, OLD_V : OLD_V + HALF].bitcast(BF16)
-            else:
-                h[c] = sbuf("h%d" % c, [P, CHUNK * PACK], BF16)[:]
-            nc.scalar.activation(h[c].rearrange("p (n t) -> p n t", t=PACK), acc[c][:].rearrange("p t n -> p n t"), GELU)
-            h_word[c] = placed("h_word%d" % c, [P, CHUNK], U32, 512 * (c % 2))
-            h_scale[c] = sbuf("h_scale%d" % c, [P, CHUNK], U8)
-            nc.vector.quantize_mx(out=h_word[c][:].bitcast(FP8X4), scales=h_scale[c][:], in_=h[c])
+        def quantise_h(name, h, tokens, offset):
+            words = placed(name + "_word", [P, tokens], U32, offset)
+            scales = sbuf(name + "_scale", [P, tokens], U8)
+            nc.vector.quantize_mx(out=words[:].bitcast(FP8X4), scales=scales[:], in_=h)
+            return words, scales
 
-        y_v = [psum.tile([P, HALF], F32, name="y_v%d" % u, tag="y_v%d" % u) for u in range(2)]
-        y_late = psum.tile([P, HALF], F32, name="y_late", tag="y_late")
-        y_s = {}
-
-        def second_product(c):
-            cols = slice(CHUNK * (c % 2), CHUNK * (c % 2 + 1))
-            if c == 0:
-                y_s[c] = psum.tile([P, CHUNK], F32, name="y_s0", tag="acc0")[:]
-            elif c == 1:
-                y_s[c] = psum.tile([P, CHUNK], F32, name="y_s1", tag="y_s1")[:]
-            else:
-                y_s[c] = y_late[:, cols]
+        def second_product(y, codes):
             for b in (1, 0):
                 nc.tensor.matmul_mx(
-                    out=y_s[c] if b == 1 else y_v[c // 2][:, cols],
+                    out=y[b],
                     lhsT=w2_word[:, 2 * P * b : 2 * P * (b + 1)].bitcast(FP4X4),
                     lhsT_scale=w2_scale[:, P * b : P * (b + 1)],
-                    rhs=h_word[c][:].bitcast(FP8X4),
-                    rhs_scale=h_scale[c][:],
+                    rhs=codes[0][:].bitcast(FP8X4),
+                    rhs_scale=codes[1][:],
                     start=True,
                     stop=True,
                 )
 
+        y = {}
+        for u in range(2):
+            for b in range(2):
+                y[u, b] = psum.tile([P, HALF], F32, name="y%d_%d" % (u, b), tag="y%d_%d" % (u, b))
         gated_v = sbuf("gated_v", [P, S], F32)
         gated_s = [sbuf("gated_s%d" % u, [P, HALF], F32) for u in range(2)]
         summed = [sbuf("summed%d" % u, [P, HALF], F32) for u in range(2)]
 
-        def gate_early(c):
-            cols = slice(CHUNK * c, CHUNK * (c + 1))
-            nc.vector.tensor_tensor(gated_s[0][:, cols], y_s[c], gates[0][:, cols], MULT)
-
-        def sum_early(c):
-            cols = slice(CHUNK * c, CHUNK * (c + 1))
-            window = rows_read[:].indirect(entries(CHUNK * c, CHUNK * (c + 1)))
-            nc.vector.tensor_tensor(summed[0][:, cols], window, gated_s[0][:, cols], ADD)
-
-        hidden(0)
-        hidden(1)
-        second_product(0)
-        second_product(1)
-        gate_early(0)
-        hidden(2)
-        sum_early(0)
-        gate_early(1)
-        hidden(3)
-        sum_early(1)
-        nc.vector.tensor_tensor(gated_v[:, 0:HALF], y_v[0][:], gates[0][:], MULT)
-        second_product(2)
-        second_product(3)
-        nc.vector.tensor_tensor(gated_s[1][:], y_late[:], gates[1][:], MULT)
-        nc.vector.tensor_tensor(gated_v[:, HALF:S], y_v[1][:], gates[1][:], MULT)
+        h0 = sbuf("h0", [P, CHUNK * PACK], BF16)[:]
+        h1 = old_v[:, OLD_V : OLD_V + HALF].bitcast(BF16)
+        h_late = sbuf("h_late", [P, HALF * PACK], BF16)
+        gelu(0, h0)
+        codes0 = quantise_h("h0", h0, CHUNK, 0)
+        gelu(1, h1)
+        codes1 = quantise_h("h1", h1, CHUNK, 512)
+        for c in range(2, CHUNKS):
+            gelu(c, h_late[:, CHUNK * PACK * (c - 2) : CHUNK * PACK * (c - 1)])
+        old_s = sbuf("old_s", [P, HALF], F32)
+        nc.vector.tensor_copy(old_s[:], rows_read[:].indirect(entries(0, HALF)))
+        second_product([y[0, b][:, 0:CHUNK] for b in range(2)], codes0)
+        second_product([y[0, b][:, CHUNK:HALF] for b in range(2)], codes1)
+        nc.vector.tensor_tensor(gated_s[0][:], y[0, 1][:], gates[0][:], MULT)
+        codes_late = quantise_h("h_late", h_late[:], HALF, 0)
+        nc.vector.tensor_tensor(summed[0][:], old_s[:], gated_s[0][:], ADD)
+        nc.vector.tensor_tensor(gated_v[:, 0:HALF], y[0, 0][:], gates[0][:], MULT)
+        second_product([y[1, b][:] for b in range(2)], codes_late)
+        nc.vector.tensor_tensor(gated_s[1][:], y[1, 1][:], gates[1][:], MULT)
+        nc.vector.tensor_tensor(gated_v[:, HALF:S], y[1, 0][:], gates[1][:], MULT)
         nc.vector.tensor_tensor(summed[1][:], rows_read[:].indirect(entries(HALF, S)), gated_s[1][:], ADD)
 
         nc.scalar.activation(old_v[:, OLD_V:S], rows_v[:].indirect(entries(OLD_V, S)), COPY)

@@ -82,10 +82,10 @@ def tile_picked_modres_mlpgelu_p_kernel(
             nc.sync.dma_start(w1_last[h][:], w1_rows[1][:, :, H // 2 * h : H // 2 * (h + 1)])
         load_x_words(1)
 
+        rows_s = sbuf("rows_s", [P, T], F32)
+        nc.sync.dma_start(rows_s[:], res[P : 2 * P, :])
         rows_v = sbuf("rows_v", [P, T], F32)
         nc.sync.dma_start(rows_v[:], res[0:P, :])
-        rows_read = sbuf("rows_read", [P, T], F32)
-        nc.sync.dma_start(rows_read[:], res[P : 2 * P, :])
         gates = [sbuf("gates%d" % u, [P, HALF], F32) for u in range(2)]
         nc.sync.dma_start(gates[0][:], gate[:, 0:HALF])
         w2_word = sbuf("w2_word", [P, 2 * N], U8)
@@ -95,8 +95,8 @@ def tile_picked_modres_mlpgelu_p_kernel(
                 w2_scale[32 * q : 32 * q + 4, :].bitcast(I32),
                 w2_scales[0][4 * q : 4 * q + 4, :].bitcast(I32),
             )
-        rows_s = sbuf("rows_s", [P, T], F32)
-        nc.sync.dma_start(rows_s[:], res[P : 2 * P, :])
+        rows_read = sbuf("rows_read", [P, T], F32)
+        nc.sync.dma_start(rows_read[:], res[P : 2 * P, :])
         nc.sync.dma_start(gates[1][:], gate[:, HALF:S])
 
         x_scale = sbuf("x_scale", [P, S], U8)
@@ -170,7 +170,8 @@ def tile_picked_modres_mlpgelu_p_kernel(
             first_product(1, c, x_word1[2][:, CHUNK * (c - 2) : CHUNK * (c - 1)])
 
         old_v = sbuf("old_v", [P, max(S, OLD_V + HALF)], F32)
-        nc.vector.tensor_copy(old_v[:, 0:OLD_V], rows_v[:].indirect(entries(0, OLD_V)))
+        old_s = sbuf("old_s", [P, HALF], F32)
+        nc.vector.tensor_copy(old_s[:], rows_s[:].indirect(entries(0, HALF)))
         def gelu(c, h):
             nc.scalar.activation(h.rearrange("p (n t) -> p n t", t=PACK), acc[c][:].rearrange("p t n -> p n t"), GELU)
 
@@ -180,44 +181,44 @@ def tile_picked_modres_mlpgelu_p_kernel(
             nc.vector.quantize_mx(out=words[:].bitcast(FP8X4), scales=scales[:], in_=h)
             return words, scales
 
-        def second_product(y, codes):
-            for b in (1, 0):
-                nc.tensor.matmul_mx(
-                    out=y[b],
-                    lhsT=w2_word[:, 2 * P * b : 2 * P * (b + 1)].bitcast(FP4X4),
-                    lhsT_scale=w2_scale[:, P * b : P * (b + 1)],
-                    rhs=codes[0][:].bitcast(FP8X4),
-                    rhs_scale=codes[1][:],
-                    start=True,
-                    stop=True,
-                )
+        def second_product(y, b, codes):
+            nc.tensor.matmul_mx(
+                out=y,
+                lhsT=w2_word[:, 2 * P * b : 2 * P * (b + 1)].bitcast(FP4X4),
+                lhsT_scale=w2_scale[:, P * b : P * (b + 1)],
+                rhs=codes[0][:].bitcast(FP8X4),
+                rhs_scale=codes[1][:],
+                start=True,
+                stop=True,
+            )
 
         y = {}
         for u in range(2):
             for b in range(2):
                 y[u, b] = psum.tile([P, HALF], F32, name="y%d_%d" % (u, b), tag="y%d_%d" % (u, b))
-        gated_v = sbuf("gated_v", [P, S], F32)
         gated_s = [sbuf("gated_s%d" % u, [P, HALF], F32) for u in range(2)]
         summed = [sbuf("summed%d" % u, [P, HALF], F32) for u in range(2)]
 
         h0 = sbuf("h0", [P, CHUNK * PACK], BF16)[:]
         h1 = old_v[:, OLD_V : OLD_V + HALF].bitcast(BF16)
-        h_late = sbuf("h_late", [P, HALF * PACK], BF16)
+        h_late = placed("h_bf16_late", [P, HALF * PACK], BF16, 1024)
         gelu(0, h0)
         codes0 = quantise_h("h0", h0, CHUNK, 0)
         gelu(1, h1)
         codes1 = quantise_h("h1", h1, CHUNK, 512)
         for c in range(2, CHUNKS):
             gelu(c, h_late[:, CHUNK * PACK * (c - 2) : CHUNK * PACK * (c - 1)])
-        old_s = sbuf("old_s", [P, HALF], F32)
-        nc.vector.tensor_copy(old_s[:], rows_read[:].indirect(entries(0, HALF)))
-        second_product([y[0, b][:, 0:CHUNK] for b in range(2)], codes0)
-        second_product([y[0, b][:, CHUNK:HALF] for b in range(2)], codes1)
+        nc.vector.tensor_copy(old_v[:, 0:OLD_V], rows_v[:].indirect(entries(0, OLD_V)))
+        for b in (1, 0):
+            second_product(y[0, b][:, 0:CHUNK], b, codes0)
+            second_product(y[0, b][:, CHUNK:HALF], b, codes1)
         nc.vector.tensor_tensor(gated_s[0][:], y[0, 1][:], gates[0][:], MULT)
         codes_late = quantise_h("h_late", h_late[:], HALF, 0)
         nc.vector.tensor_tensor(summed[0][:], old_s[:], gated_s[0][:], ADD)
+        gated_v = placed("gated_v", [P, S], F32, 1024)
         nc.vector.tensor_tensor(gated_v[:, 0:HALF], y[0, 0][:], gates[0][:], MULT)
-        second_product([y[1, b][:] for b in range(2)], codes_late)
+        for b in (1, 0):
+            second_product(y[1, b][:], b, codes_late)
         nc.vector.tensor_tensor(gated_s[1][:], y[1, 1][:], gates[1][:], MULT)
         nc.vector.tensor_tensor(gated_v[:, HALF:S], y[1, 0][:], gates[1][:], MULT)
         nc.vector.tensor_tensor(summed[1][:], rows_read[:].indirect(entries(HALF, S)), gated_s[1][:], ADD)

from contextlib import ExitStack

import concourse.mybir as mybir

K, T, S, H, N = 1024, 1024, 512, 512, 256
FLOPS = 2 * S * (K * H + H * N)

P = 128
PACK = 4
QUADRANTS = 4
CHUNK = 128
CHUNKS = S // CHUNK
HALF = S // 2

F32 = mybir.dt.float32
BF16 = mybir.dt.bfloat16
I32 = mybir.dt.int32
U32 = mybir.dt.uint32
U16 = mybir.dt.uint16
U8 = mybir.dt.uint8
FP8X4 = mybir.dt.float8_e4m3fn_x4
FP4X4 = mybir.dt.float4_e2m1fn_x4
GELU = mybir.ActivationFunctionType.Gelu_apprx_tanh
COPY = mybir.ActivationFunctionType.Copy
ADD = mybir.AluOpType.add
MULT = mybir.AluOpType.mult


def tile_picked_modres_mlpgelu_p_kernel(
    tc, x_words, x_scales, gate, res, w1, w2_words, w2_scales, offs, out
):
    nc = tc.nc
    with ExitStack() as ctx:
        keep = ctx.enter_context(tc.tile_pool(name="keep", bufs=1))
        by_hand = ctx.enter_context(tc.tile_pool(name="by_hand", bufs=1))
        psum = ctx.enter_context(tc.psum_pool(name="psum", bufs=1))

        def sbuf(name, shape, dtype):
            return keep.tile(shape, dtype, name=name, align_bytes=256)

        def placed(name, shape, dtype, offset):
            return by_hand.tile(shape, dtype, name=name, offset=offset, align_bytes=64)

        OLD_V = 192
        x_scale_window = sbuf("x_scale_window", [P, T], U8)
        nc.gpsimd.memset(x_scale_window[:].bitcast(I32), 0)

        def load_x_scales(queue, q):
            queue.dma_start(
                x_scale_window[32 * q : 32 * q + 8, :].bitcast(I32),
                x_scales[:, 4 * q : 4 * q + 4, :].bitcast(I32),
            )

        for q in range(2):
            load_x_scales(nc.scalar, q)
        table_in = sbuf("table_in", [P, 16], F32)
        table_out = sbuf("table_out", [P, 16], F32)
        nc.gpsimd.memset(table_in[:], 0.0)
        nc.scalar.activation(table_out[:], table_in[:], GELU)
        w2_scale = sbuf("w2_scale", [P, N], U8)
        nc.gpsimd.memset(w2_scale[:].bitcast(I32), 0)

        offsets = sbuf("offsets", [P, S // 16], U16)

        def entries(lo, hi):
            return offsets[:, lo // 16 : hi // 16]

        x_window = [sbuf("x_window%d" % g, [P, T], U32) for g in range(2)]

        def load_x_words(g):
            nc.sync.dma_start(x_window[g][:].bitcast(I32), x_words[g].rearrange("p n j -> p (n j)").bitcast(I32))

        load_x_words(0)
        nc.sync.dma_start(offsets[:], offs)
        for q in range(2, QUADRANTS):
            load_x_scales(nc.sync, q)
        w1_rows = w1.rearrange("(g p j) c -> g p j c", g=2, j=PACK)
        w1_first = sbuf("w1_first", [P, PACK, H], F32)
        nc.sync.dma_start(w1_first[:], w1_rows[0])
        w1_last = [sbuf("w1_last%d" % h, [P, PACK, H // 2], F32) for h in range(2)]
        for h in range(2):
            nc.sync.dma_start(w1_last[h][:], w1_rows[1][:, :, H // 2 * h : H // 2 * (h + 1)])
        load_x_words(1)

        rows_s = sbuf("rows_s", [P, T], F32)
        nc.sync.dma_start(rows_s[:], res[P : 2 * P, :])
        rows_v = sbuf("rows_v", [P, T], F32)
        nc.sync.dma_start(rows_v[:], res[0:P, :])
        gates = [sbuf("gates%d" % u, [P, HALF], F32) for u in range(2)]
        nc.sync.dma_start(gates[0][:], gate[:, 0:HALF])
        w2_word = sbuf("w2_word", [P, 2 * N], U8)
        nc.sync.dma_start(w2_word[:].bitcast(I32), w2_words[0].bitcast(I32))
        for q in range(QUADRANTS):
            nc.sync.dma_start(
                w2_scale[32 * q : 32 * q + 4, :].bitcast(I32),
                w2_scales[0][4 * q : 4 * q + 4, :].bitcast(I32),
            )
        rows_read = sbuf("rows_read", [P, T], F32)
        nc.sync.dma_start(rows_read[:], res[P : 2 * P, :])
        nc.sync.dma_start(gates[1][:], gate[:, HALF:S])

        x_scale = sbuf("x_scale", [P, S], U8)
        nc.vector.tensor_copy(x_scale[:], x_scale_window[:].indirect(offsets[:]))
        x_word0 = sbuf("x_word0", [P, S], U32)
        nc.vector.tensor_copy(x_word0[:], x_window[0][:].indirect(offsets[:]))

        acc = [psum.tile([P, PACK, CHUNK], F32, name="acc%d" % c, tag="acc%d" % c) for c in range(CHUNKS)]
        w1_word = {}
        w1_scale = {}
        for g in range(2):
            for u in range(2):
                w1_word[g, u] = sbuf("w1_word%d_%d" % (g, u), [P, 2 * P], U32)
                w1_scale[g, u] = sbuf("w1_scale%d_%d" % (g, u), [P, 2 * P], U8)

        def round_pairs(name, raw, units):
            src = raw[:].rearrange("p j (m t) -> p m j t", t=PACK)
            pairs = [sbuf("%s_%d" % (name, u), [P, 2, units, PACK], BF16) for u in range(2)]
            nc.vector.tensor_copy(pairs[0][:].rearrange("p t m j -> p m j t"), src[:, :, :, 0:2])
            nc.scalar.copy(pairs[1][:].rearrange("p t m j -> p m j t"), src[:, :, :, 2:4])
            return pairs

        def quantise_first(u, pairs):
            nc.vector.quantize_mx(
                out=w1_word[0, u][:].bitcast(FP8X4),
                scales=w1_scale[0, u][:],
                in_=pairs[u][:].rearrange("p t m j -> p (t m j)"),
            )

        def quantise_last(h, u, pairs):
            for t in range(2):
                cols = slice(P * t + 64 * h, P * t + 64 * (h + 1))
                nc.vector.quantize_mx(
                    out=w1_word[1, u][:, cols].bitcast(FP8X4),
                    scales=w1_scale[1, u][:, cols],
                    in_=pairs[u][:, t].rearrange("p m j -> p (m j)"),
                )

        def first_product(g, c, words):
            for t in range(PACK):
                units = slice(P * (t % 2), P * (t % 2 + 1))
                nc.tensor.matmul_mx(
                    out=acc[c][:, t, :],
                    lhsT=w1_word[g, t // 2][:, units].bitcast(FP8X4),
                    lhsT_scale=w1_scale[g, t // 2][:, units],
                    rhs=words.bitcast(FP8X4),
                    rhs_scale=x_scale[4 * g : P, CHUNK * c : CHUNK * (c + 1)],
                    start=(g == 0 and t == 0),
                    stop=(g == 1 and t == PACK - 1),
                )

        first = round_pairs("w1_bf16_first", w1_first, P)
        quantise_first(0, first)
        last0 = round_pairs("w1_bf16_last0", w1_last[0], 64)
        quantise_first(1, first)
        for c in range(CHUNKS):
            first_product(0, c, x_word0[:, CHUNK * c : CHUNK * (c + 1)])
        quantise_last(0, 0, last0)
        last1 = round_pairs("w1_bf16_last1", w1_last[1], 64)
        quantise_last(0, 1, last0)
        quantise_last(1, 0, last1)
        quantise_last(1, 1, last1)

        x_word1 = [sbuf("x_word1_%d" % i, [P, n], U32) for i, n in enumerate((CHUNK, CHUNK, HALF))]
        nc.vector.tensor_copy(x_word1[0][:], x_window[1][:].indirect(entries(0, CHUNK)))
        first_product(1, 0, x_word1[0][:])
        nc.vector.tensor_copy(x_word1[1][:], x_window[1][:].indirect(entries(CHUNK, HALF)))
        first_product(1, 1, x_word1[1][:])
        nc.vector.tensor_copy(x_word1[2][:], x_window[1][:].indirect(entries(HALF, S)))
        for c in range(2, CHUNKS):
            first_product(1, c, x_word1[2][:, CHUNK * (c - 2) : CHUNK * (c - 1)])

        old_v = sbuf("old_v", [P, max(S, OLD_V + HALF)], F32)
        old_s = sbuf("old_s", [P, HALF], F32)
        nc.vector.tensor_copy(old_s[:], rows_s[:].indirect(entries(0, HALF)))
        def gelu(c, h):
            nc.scalar.activation(h.rearrange("p (n t) -> p n t", t=PACK), acc[c][:].rearrange("p t n -> p n t"), GELU)

        def quantise_h(name, h, tokens, offset):
            words = placed(name + "_word", [P, tokens], U32, offset)
            scales = sbuf(name + "_scale", [P, tokens], U8)
            nc.vector.quantize_mx(out=words[:].bitcast(FP8X4), scales=scales[:], in_=h)
            return words, scales

        def second_product(y, b, codes):
            nc.tensor.matmul_mx(
                out=y,
                lhsT=w2_word[:, 2 * P * b : 2 * P * (b + 1)].bitcast(FP4X4),
                lhsT_scale=w2_scale[:, P * b : P * (b + 1)],
                rhs=codes[0][:].bitcast(FP8X4),
                rhs_scale=codes[1][:],
                start=True,
                stop=True,
            )

        y = {}
        for u in range(2):
            for b in range(2):
                y[u, b] = psum.tile([P, HALF], F32, name="y%d_%d" % (u, b), tag="y%d_%d" % (u, b))
        gated_s = [sbuf("gated_s%d" % u, [P, HALF], F32) for u in range(2)]
        summed = [sbuf("summed%d" % u, [P, HALF], F32) for u in range(2)]

        h0 = sbuf("h0", [P, CHUNK * PACK], BF16)[:]
        h1 = old_v[:, OLD_V : OLD_V + HALF].bitcast(BF16)
        h_late = placed("h_bf16_late", [P, HALF * PACK], BF16, 1024)
        gelu(0, h0)
        codes0 = quantise_h("h0", h0, CHUNK, 0)
        gelu(1, h1)
        codes1 = quantise_h("h1", h1, CHUNK, 512)
        for c in range(2, CHUNKS):
            gelu(c, h_late[:, CHUNK * PACK * (c - 2) : CHUNK * PACK * (c - 1)])
        nc.vector.tensor_copy(old_v[:, 0:OLD_V], rows_v[:].indirect(entries(0, OLD_V)))
        for b in (1, 0):
            second_product(y[0, b][:, 0:CHUNK], b, codes0)
            second_product(y[0, b][:, CHUNK:HALF], b, codes1)
        nc.vector.tensor_tensor(gated_s[0][:], y[0, 1][:], gates[0][:], MULT)
        codes_late = quantise_h("h_late", h_late[:], HALF, 0)
        nc.vector.tensor_tensor(summed[0][:], old_s[:], gated_s[0][:], ADD)
        gated_v = placed("gated_v", [P, S], F32, 1024)
        nc.vector.tensor_tensor(gated_v[:, 0:HALF], y[0, 0][:], gates[0][:], MULT)
        for b in (1, 0):
            second_product(y[1, b][:], b, codes_late)
        nc.vector.tensor_tensor(gated_s[1][:], y[1, 1][:], gates[1][:], MULT)
        nc.vector.tensor_tensor(gated_v[:, HALF:S], y[1, 0][:], gates[1][:], MULT)
        nc.vector.tensor_tensor(summed[1][:], rows_read[:].indirect(entries(HALF, S)), gated_s[1][:], ADD)

        nc.scalar.activation(old_v[:, OLD_V:S], rows_v[:].indirect(entries(OLD_V, S)), COPY)
        for u in range(2):
            nc.scalar.activation(rows_s[:].indirect(entries(HALF * u, HALF * (u + 1))), summed[u][:], COPY)
        nc.scalar.dma_start(out[P : 2 * P, :], rows_s[:])

        nc.vector.tensor_tensor(rows_v[:].indirect(offsets[:]), gated_v[:], old_v[:, 0:S], ADD)
        nc.sync.dma_start(out[0:P, :], rows_v[:])
